import numpy as np, ml_dtypes
CORES = [3,11,19,27,35,43,51,59]
N = 8
import mx_ref
BF = ml_dtypes.bfloat16
def entries(a):
    return np.ascontiguousarray(a.T).reshape(-1)
def table(e):
    return np.ascontiguousarray(np.reshape(e, (-1, 16)).T).astype(np.int32)
def pick(q, e):
    c = np.concatenate([q[0].reshape(128, -1, 4), np.zeros((128, 1, 4), np.uint8)], axis=1); s = np.concatenate([q[1], np.ones((16, 1), np.uint8)], axis=1)
    return (np.ascontiguousarray(c[:, e].reshape(128, -1)), np.ascontiguousarray(s[:, e]))
def join(*qs):
    return (np.concatenate([q[0] for q in qs], axis=1), np.concatenate([q[1] for q in qs], axis=1))
def put(q, e, v):
    c, s = q[0].reshape(128, -1, 4).copy(), q[1].copy(); c[:, e] = v[0].reshape(128, -1, 4); s[:, e] = v[1]
    return (c.reshape(128, -1), s)
def pk(c, s):
    return (np.ascontiguousarray(c), mx_ref.live(s))
def emit(q):
    return q[0], q[1]
def cols(t, e):
    v = np.concatenate([t.reshape(128, -1, 4), np.zeros((128, 1, 4), BF)], axis=1)
    return np.ascontiguousarray(v[:, e]).reshape(128, -1)
def cut(t, i, w=512):
    return t[:, w * i:w * i + w]
def f(rng, *shape):
    return mx_ref.flush((rng.standard_normal(shape, dtype=np.float32) * np.exp2(rng.integers(-2, 3, shape[:-1] + (1,)))).astype(BF))
def wide(rng, *shape, cols=0):
    v = rng.standard_normal(shape, dtype=np.float32) * np.exp2(rng.integers(-12, 13, shape)).astype(np.float32)
    if cols: v *= np.repeat(np.exp2(rng.integers(-cols, cols + 1, shape[:-2] + (1, shape[-1] // 4))) * (rng.random(shape[:-2] + (1, shape[-1] // 4)) > 0.0625), 4, axis=-1).astype(np.float32)
    return mx_ref.flush(v.astype(BF))
P, CAPP, LC = 256, 32, 128
def choose(e, g, d):
    c = e[np.arange(P), np.argmax(g[e], axis=1)]
    for s in range(N):
        if s != d:
            late = np.flatnonzero(c // P == s)[CAPP:]
            c[late] = e[late, 0]
    return c
def play(e0, e1, e2, p1, p2, u, a):
    k = [mx_ref.quantize(u[d]) for d in range(N)]
    A = [[mx_ref.quantize(np.ascontiguousarray(cut(a[d], i))) for i in range(4)] for d in range(N)]
    H = [mx_ref.quantize(e0[d]) for d in range(N)]
    g = np.stack([mx_ref.matmul(k[d], H[d])[0] for d in range(N)]) + np.float32(0)
    chosen, tiles, scores = [], [], [g]
    for e, p in ((e1, p1), (e2, p2)):
        every, before = join(*H), g.reshape(-1)
        H, g = [], np.zeros((N, P), np.float32)
        for d in range(N):
            c = choose(entries(p[d]).reshape(P, 4), before, d)
            x = pick(every, c)
            R = np.stack([mx_ref.matmul(A[d][i], x) for i in range(4)], axis=2).reshape(128, 4 * P)
            h = (R * np.float32(0.05) + e[d].astype(np.float32)).astype(BF)
            q = mx_ref.quantize(h)
            g[d] = before[c] + mx_ref.matmul(k[d], q)[0]
            H.append(q)
            chosen.append(c)
            tiles.append(h)
        scores.append(g)
    return np.stack(chosen).reshape(2, N, P), tiles, scores, H
def large(v):
    v = v.astype(np.float32)
    v[np.abs(v) < np.float32(0.03125)] = 0
    return v.astype(BF)
def lean(v, u, s):
    t = np.abs(v.astype(np.float32)).reshape(128, -1, 4) * np.sign(u[:, None, :4].astype(np.float32)) * np.asarray(s, np.float32)[None, :, None]
    return t.reshape(128, -1).astype(BF)
def near(t, u, score):
    size = np.concatenate([[0.0], np.exp2(np.arange(-26, -7))])[:, None] * np.array([1, 1.25, 1.5, 1.75])
    v = np.repeat(t.astype(np.float32).reshape(128, 1, 4), 80, axis=1)
    v[:8] = np.sign(u[:8, None, :4].astype(np.float32)) * size.reshape(1, 80, 1)
    v = np.ascontiguousarray(v.reshape(128, 320).astype(BF))
    s = score(v)
    i = int(np.argmin(np.abs(s - s[0] - np.float32(2.5) * np.spacing(np.abs(s[0])))))
    return cols(v, [0, i])
def strong(u):
    return (u.astype(np.float32) * np.float32(2.0 ** 24)).astype(BF)
def lists(rng):
    out = []
    for d in range(N):
        others = np.delete(np.arange(N), d)
        rank = others[np.argsort(rng.random((P, N - 1)), axis=1)[:, :3]]
        pool = np.stack([rng.permutation(P)[:LC] for s in range(N)])
        e = np.zeros((P, 4), int)
        e[:, 0] = d * P + rng.integers(0, P, P)
        e[:, 1:] = rank * P + pool[rank, rng.integers(0, LC, (P, 3))]
        out.append(table(e.reshape(-1)))
    return np.stack(out)
def crowd(rng, s):
    out, half = [], LC // 2
    for d in range(N):
        x = rng.permutation(np.delete(np.arange(N), d))
        hi = np.stack([rng.permutation(np.flatnonzero(s[r]))[:half] for r in range(N)])
        lo = np.stack([rng.permutation(np.flatnonzero(~s[r]))[:half] for r in range(N)])
        j = rng.permutation(P)
        one, two, home = j[:P // 2], j[P // 2:P // 2 + CAPP], j[P // 2 + CAPP:]
        rank = np.stack([np.full(P, x[0]), np.full(P, x[1]), x[rng.integers(2, N - 1, P)]], axis=1)
        n = rng.integers(0, half, (P, 3))
        n[j, 0] = np.arange(P) % (P // 2) % half
        n[two, 1] = rng.permutation(half)[:CAPP]
        at = lo[rank, n]
        at[one, 0] = hi[x[0], n[one, 0]]
        at[two, 1] = hi[x[1], n[two, 1]]
        e = np.zeros((P, 4), int)
        e[:, 0] = d * P + np.flatnonzero(~s[d])[rng.integers(0, P // 2, P)]
        e[home, 0] = d * P + np.flatnonzero(s[d])[rng.integers(0, P // 2, home.size)]
        e[:, 1:] = rng.permuted(rank * P + at, axis=1)
        out.append(table(e.reshape(-1)))
    return np.stack(out)
def plain(rng):
    u = np.array(f(rng, 128, 512))
    u[:, 4:] = 0
    return {"e0": np.array(f(rng, N, 128, 4 * P)), "e1": large(f(rng, N, 128, 4 * P)), "e2": large(f(rng, N, 128, 4 * P)), "p1": lists(rng), "p2": lists(rng),
            "u": np.stack([u] * N), "a": f(rng, N, 128, 2048), "w": f(rng, N, 128, 512)}
def setup_inputs(rng):
    return plain(rng)
def setup_inputs_full(rng):
    d = plain(rng)
    for e, p, size in (("e0", "p1", 1), ("e1", "p2", 64)):
        s = np.stack([rng.permutation(P) < P // 2 for r in range(N)])
        for r in range(N): d[e][r] = lean(d[e][r], d["u"][r], size * np.where(s[r], 1, -1))
        d[p] = crowd(rng, s)
    return d
def setup_inputs_ties(rng):
    d = plain(rng)
    u, a = np.ascontiguousarray(d["u"][0]), np.array(d["a"][0])
    a.reshape(128, 4, 512)[:, :, :32] = 0
    k = mx_ref.quantize(u)
    def row(t): return mx_ref.matmul(k, mx_ref.quantize(t))[0]
    x = np.concatenate([f(rng, 128, 16), near(lean(f(rng, 128, 4), u, [1]), u, row)], axis=1)
    best = cols(x, [5] * 4)
    top, q = row(best)[0], mx_ref.quantize(best)
    R = np.stack([mx_ref.matmul(mx_ref.quantize(np.ascontiguousarray(cut(a, i))), q)[:, 0] for i in range(4)], axis=1)
    def later(t): return top + row((np.tile(R, 80) * np.float32(0.05) + t.astype(np.float32)).astype(BF))
    z = near(lean(large(f(rng, 128, 4)), u, [8]), u, later)
    d["e0"] = np.stack([cols(x, rng.integers(0, 6, P)) for r in range(N)])
    d["e1"] = np.stack([cols(z, rng.integers(0, 2, P)) for r in range(N)])
    d["a"] = np.stack([a] * N)
    return d
def setup_inputs_own(rng):
    d = plain(rng)
    d["u"] = strong(d["u"])
    best, worst = rng.permutation(N)[:2]
    for r, s in ((best, 1), (worst, -1)):
        d["e0"][r] = lean(d["e0"][r], d["u"][r], np.full(P, 8 * s))
        d["e1"][r] = lean(d["e1"][r], d["u"][r], np.full(P, 256 * s))
    return d
def setup_inputs_flip(rng):
    d = plain(rng)
    d["u"] = strong(d["u"])
    for r in range(N):
        s = rng.permutation(P) % 2 * 2 - 1
        d["e0"][r] = lean(d["e0"][r], d["u"][r], 1024 * s)
        d["e1"][r] = lean(d["e1"][r], d["u"][r], -16384 * s)
    return d
def setup_inputs_spread(rng):
    d = plain(rng)
    d["e0"] = wide(rng, N, 128, 4 * P, cols=4)
    d["e1"] = large(wide(rng, N, 128, 4 * P, cols=4))
    d["e2"] = large(wide(rng, N, 128, 4 * P, cols=4))
    return d
def check_inputs(d):
    b = []
    for k in ("e0", "e1", "e2", "u", "a", "w"):
        v = np.abs(d[k].astype(np.float32))
        if not (np.isfinite(v).all() and ((v == 0) | (v >= 2.0 ** -30) & (v <= 2.0 ** 30)).all()): b.append("a value of " + k)
    u = d["u"].astype(np.float32)
    if (u[:, :, 4:] != 0).any(): b.append("u has numbers behind its column 0")
    if (u != u[:1]).any(): b.append("u isn't the same on all ranks")
    for k in ("p1", "p2"):
        for r in range(N):
            e = entries(d[k][r]).reshape(P, 4)
            if e.min() < 0 or e.max() >= N * P:
                b.append(k + " out of range")
                continue
            o = np.sort(e[:, 1:] // P, axis=1)
            if (e[:, 0] // P != r).any(): b.append(k + ": predecessor 0")
            if (o == r).any() or (o[:, 1:] == o[:, :-1]).any(): b.append(k + ": predecessors 1 to 3")
            if np.bincount(np.unique(e[:, 1:]) // P, minlength=N).max() > LC: b.append(k + ": too many columns of one rank")
    if not b:
        chosen, tiles, scores, H = play(*[d[k] for k in ("e0", "e1", "e2", "p1", "p2", "u", "a")])
        v = np.abs(np.stack(tiles).astype(np.float32))
        if not (np.isfinite(v).all() and ((v == 0) | (v >= 2.0 ** -30) & (v <= 2.0 ** 30)).all()): b.append("a value of h_1 or h_2")
        if not np.isfinite(np.stack(scores)).all(): b.append("a score")
    return b
def reference(e0, e1, e2, p1, p2, u, a, w):
    chosen, tiles, scores, H = play(e0, e1, e2, p1, p2, u, a)
    ch, g = np.zeros((N, 2, P), np.float32), np.zeros((N, 1, P), np.float32)
    oc, osc, y = np.zeros((N, 128, 4 * P), np.uint8), np.zeros((N, 16, P), np.uint8), np.zeros((N, 128, P), np.float32)
    for r in range(N):
        ch[r] = chosen[:, r]
        g[r, 0] = scores[2][r]
        oc[r], osc[r] = emit(H[r])
        y[r] = mx_ref.matmul(mx_ref.quantize(w[r]), H[r])
    return {"ch": ch, "g": g, "oc": oc, "osc": osc, "y": y}

@@ -1,0 +1,451 @@
+from concourse.bass import DstId, RemoteDMATransfer
+from concourse.mybir import dt, AluOpType as A, AxisListType, ActivationFunctionType as F
+
+N, P, CAP = 8, 256, 32
+HALF = P // 2
+PIECES = 2
+BIG = 9e29
+U = 1.0 / 4096.0
+
+_f32, _i32, _u16, _bf = "float32", "int32", "uint16", "bfloat16"
+SCRATCH = {"ps": ("psum", [128, 2048], _f32), "pr": ("psum", [128, 2048], _f32), "sld1": ("dram", [8, 128, 2], _f32), "sld2": ("dram", [8, 128, 2], _f32)}
+for _d, _l in (
+        (_bf, "e0t 1024 e1t 1024 e2t 1024 ut 512 at 2048 wt 512 h1 1024 h2 1024"),
+        (_f32, "tm1 1024 tm2 1024 sc 2048 iot 2048 rs 512 rsb 512 zer 256 ta 32 sb 32 tb 32 nq 128 cc1 128 cct1 128 cx1 128 cr1 128 "
+               "cc2 128 cct2 128 cx2 256 cr2 288 fc 16 d0 256 d1 256 rv 2 scr1 256 scr2 256 scc 2 g0c 2 g1c 2 chr1 256 chr2 256 go 256 ys 256 "
+               "mc 128 mn 128 exm 256 k2 128 nx2 256 nt2 256 dc 256 zz2 256"),
+        (_i32, "pt 64 pa 64 np 64 lo 64 hb 64 tl 64 hm 64 po 64 iz 16 ij 8 ic 8 iy 32 ti 256 tj 256"),
+        (_u16, "of 64 op 64 rj 16 rh 8 dup 32 dup4 32 rq 2 rqs 16 ofq 16 ofx1 16 ofs1 16 ofa1 16 ofx2 16 ofs2 16 ofa2 16")):
+    _w = _l.split()
+    for _k in range(0, len(_w), 2):
+        SCRATCH[_w[_k]] = ("sbuf", [128, int(_w[_k + 1])], _d)
+for _n, _c in (("uq", 128), ("aq", 512), ("wq", 128), ("hw", 2048), ("hr", 256), ("x1", 256), ("hq", 256), ("sp", 224), ("w2", 512), ("x2", 256),
+               ("zq", 256)):
+    SCRATCH[_n] = ("sbuf", [128, _c], "float8_e4m3fn_x4")
+    SCRATCH[_n + "s"] = ("sbuf", [128, _c], "uint8")
+for _t in ("1", "2"):
+    for _n, _c in (("ga", 512), ("mx", 512), ("fl", 512), ("cn", 512), ("nr", 512), ("vd", 512),
+                   ("ad", 256), ("mk", 256), ("ct", 256), ("ex", 512), ("tr", 512), ("mr", 512)):
+        SCRATCH[_n + _t] = ("sbuf", [128, _c], _f32)
+
+SEMAPHORES = ["cv", "cs", "ct", "cg", "l0", "ls", "r0", "rg", "rr", "rc", "hk"] + ["h%d" % i for i in range(N)] + ["hc%d" % i for i in range(PIECES)]
+SEMAPHORES += ["de0", "du", "dp1", "dp2", "da", "de1", "dw", "de2", "dog0", "dog1", "ds0", "ds1", "ds2", "ds3", "dsc", "dofq", "dofs", "dch", "dout"]
+
+
+def bits(m):
+    return bin(m).count("1")
+
+
+def plan(d, cores, topo):
+    me = cores[d]
+    here = topo.chip(me)
+    order = sorted([i for i in range(N) if i != d], key=lambda i: (-min((i - d) % N, (d - i) % N), (i - d) % N))
+    mate = [i for i in order if topo.mates(here, topo.chip(cores[i]))]
+    plane = [i for i in order if topo.same_plane(here, topo.chip(cores[i]))]
+    far = [i for i in order if i not in mate + plane]
+    used, out = [me], []
+    for same, ranks in ((True, far[2:] + mate), (True, plane[1:]), (False, far[:1] + plane[:1]), (False, far[1:2])):
+        able = [h for h in topo.cores_of(me) if h not in used and (topo.die(h) == topo.die(me)) == same and all(topo.may_write(h, cores[i]) for i in ranks)]
+        able.sort(key=lambda h: sum(topo.may_write(h, cores[i]) for i in order))
+        used.append(able[0])
+        out.append((able[0], ranks))
+    return [(h, r, out[k + 1][0] if k % 2 == 0 else None) for k, (h, r) in enumerate(out)]
+
+
+def chip_engines(topo, core, near, far):
+    return topo.mask(core, near) & ~topo.mask(core, far)
+
+
+def pieces(T):
+    w = P // PIECES
+    out = []
+    for k in range(PIECES):
+        out.append(("hc%d" % k, T.hr[:, w * k:w * k + w].bitcast(dt.uint8), lambda q, k=k: T.hw[:, P * q + w * k:P * q + w * k + w].bitcast(dt.uint8)))
+    out.append(("hk", T.hrs[:], lambda q: T.hws[:, P * q:P * q + P]))
+    return out
+
+
+def dst_of(topo, c):
+    rid, pid, _ = topo.addr(c)
+    return DstId(rid=rid, pnc=pid)
+
+
+def hand_on(g, core, T, topo):
+    for d in range(N):
+        for h, ranks, sub in plan(d, T.cores, topo):
+            if h != core:
+                continue
+            far = T.cores[ranks[0]]
+            mask = topo.mask(core, far)
+            came = bits(chip_engines(topo, T.cores[d], core, far))
+            n = 0
+            for sem, here, land in pieces(T):
+                g.wait_ge(T.sem[sem], came)
+                ts = [RemoteDMATransfer(dst_ids=[dst_of(topo, T.cores[i]) for i in ranks], dma_engine_mask=mask, remote_sem=T.sem["h%d" % d], srcs=[here],
+                                        dsts=[land((d - i) % N) for i in ranks])]
+                n += bits(mask)
+                if sub is not None:
+                    m = chip_engines(topo, core, sub, far)
+                    ts.insert(0, RemoteDMATransfer(dst_ids=[dst_of(topo, sub)], dma_engine_mask=m, remote_sem=T.sem[sem], srcs=[here], dsts=[here]))
+                    n += bits(m)
+                g.remote_dma_fused(ts, local_sem=T.sem.ls)
+            g.wait_ge(T.sem.ls, n)
+
+
+def rank_program(g, core, T, topo):
+    d = T.rank_of(core)
+    if d is None:
+        hand_on(g, core, T, topo)
+        return
+    cores = T.cores
+    Q = {"v": g.vector, "s": g.scalar, "t": g.tensor, "g": g, "y": g.sync}
+    total, seen = {}, {}
+
+    def wait(q, deps):
+        need = {}
+        for name, val in deps:
+            need[name] = max(val, need.get(name, 0))
+        for name in need:
+            if seen.get((q, name), 0) < need[name]:
+                Q[q].wait_ge(T.sem[name], need[name])
+                seen[(q, name)] = need[name]
+
+    def note(ins, name, n):
+        ins.then_inc(T.sem[name], n)
+        total[name] = total.get(name, 0) + n
+        return (name, total[name])
+
+    def V(call, deps, *args, **kw):
+        wait("v", deps)
+        return note(call(*args, **kw), "cv", 1)
+
+    def S(deps, *args, **kw):
+        wait("s", deps)
+        return note(g.scalar.activation(*args, **kw), "cs", 1)
+
+    def MM(deps, out, w, ws, x, xs):
+        wait("t", deps)
+        return note(g.tensor.matmul_mx(out, w, ws, x, xs, True, True), "ct", 1)
+
+    def G(call, deps, *args, **kw):
+        wait("g", deps)
+        return note(call(*args, **kw), "cg", 1)
+
+    def D(q, deps, name, out, in_):
+        wait(q, deps)
+        return note(Q[q].dma_start(out, in_), name, 16)
+
+    tt, ts, tc = g.vector.tensor_tensor, g.vector.tensor_scalar, g.vector.tensor_copy
+    ms, qz, scan, red, tp = g.vector.memset, g.vector.quantize_mx, g.vector.tensor_tensor_scan, g.vector.tensor_reduce, g.vector.transpose
+    u8, u32 = dt.uint8, dt.uint32
+
+    others = [(d + k) % N for k in range(1, N)]
+    all_ = [cores[i] for i in others]
+    mask = topo.mask(core, all_[0])
+    for c in all_:
+        mask &= topo.mask(core, c)
+    engs = [e for e in topo.engines(core, all_[0]) if mask >> e & 1]
+    neng = len(engs)
+    helpers = [h for h, r, sub in plan(d, cores, topo)][0::2]
+    inner = chip_engines(topo, core, helpers[0], all_[0])
+
+    def sent(name, n):
+        total[name] = total.get(name, 0) + n
+        return (name, total[name])
+
+    def send(deps, sem, src, to, dsts, local="ls", m=mask):
+        wait("g", deps)
+        g.remote_dma_fused([RemoteDMATransfer(dst_ids=[dst_of(topo, c) for c in to], dma_engine_mask=m, remote_sem=T.sem[sem], srcs=[src], dsts=dsts)],
+                           local_sem=T.sem[local])
+        return sent(local, bits(m))
+
+    def send_each(deps, sem, pairs):
+        wait("g", deps)
+        g.remote_dma_fused([RemoteDMATransfer(dst_ids=[dst_of(topo, all_[k])], dma_engine_mask=1 << engs[k], remote_sem=T.sem[sem], srcs=[a], dsts=[b])
+                            for k, (a, b) in enumerate(pairs)], local_sem=T.sem.ls)
+        return sent("ls", len(pairs))
+
+    def rel(s, r):
+        return (s - r) % N
+
+    e0 = D("y", [], "de0", T.e0t[:], T.e0[:, :])
+    uu = D("s", [], "du", T.ut[:], T.u[:, :])
+    for k in range(8):
+        p1 = D("y", [], "dp1", T.pt[16 * k:16 * k + 16, 0:32], T.p1[:, 32 * (k % 2):32 * (k % 2) + 32])
+    da = D("y", [], "da", T.at[:], T.a[:, :])
+
+    gi = G(g.iota, [], T.iot[:, 0:512], [[1, 512]], 0, 0, allow_small_or_imprecise_dtypes=True)
+    gp = G(g.iota, [], T.ic[:, 0:1], [[0, 1]], 0, 1)
+    giy = G(g.iota, [], T.iy[:], [[16, 16], [0, 2]], 0, 0)
+    giz = G(g.iota, [], T.iz[:], [[16, 2], [32, 4], [0, 2]], 0, 0)
+    gij = G(g.iota, [], T.ij[:], [[16, 8]], 0, 0)
+    c0 = V(ms, [], T.sc[:, 0:512], 0.0)
+    zr = V(ms, [], T.zer[:], 0.0)
+    r1 = V(ms, [], T.rs[:], BIG)
+    for k in (1, 2, 3):
+        sc0 = S([c0], T.sc[:, 512 * k:512 * k + 512], T.sc[:, 0:512], F.Copy)
+    for k in (1, 2, 3):
+        io = S([gi], T.iot[:, 512 * k:512 * k + 512], T.iot[:, 0:512], F.Identity, bias=512.0 * k)
+    rs = V(ms, [r1], T.rs[:, 0:512:4], -BIG)
+
+    q0 = V(qz, [e0], T.hw[:, 0:P], T.hws[:, 0:P], T.e0t[:])
+    quq = V(qz, [uu], T.uq[:], T.uqs[:], T.ut[:])
+
+    def scores(deps, w, ws, ps):
+        return MM(deps + [quq], ps, w, ws, T.uq[:], T.uqs[:])
+
+    for k in (0, 1):
+        m = scores([q0], T.hw[:, HALF * k:HALF * k + HALF], T.hws[:, HALF * k:HALF * k + HALF], T.ps[:, 512 * k:512 * k + 128])
+    g0 = V(tc, [m], T.g0c[:], T.ps[:, 0:1024:512])
+    parts = pieces(T)
+    send([q0], parts[0][0], parts[0][2](0), helpers, [parts[0][1]] * 2, "l0", inner)
+    send([g0], "r0", T.g0c[:], all_, [T.sld1[rel(d, i)] for i in others])
+    for sem, there, here in parts[1:]:
+        send([q0], sem, here(0), helpers, [there] * 2, "l0", inner)
+    og = D("y", [g0], "dog0", T.sld1[0], T.g0c[:])
+
+    def places(n, lo, hb, tl, hm, po):
+        a1 = V(ts, [n[0]], lo, n[1], 127, None, A.bitwise_and)
+        a2 = V(ts, [n[0]], hb, n[1], 7, 1, A.logical_shift_right, A.bitwise_and)
+
+        def rest():
+            a3 = V(tt, [a1], tl, n[1], lo, A.add)
+            a4 = V(ts, [a2], hm, hb, -127.0, None, A.mult)
+            return V(tt, [a3, a4], po, tl, hm, A.add)
+        return rest
+
+    def listed(t, dep):
+        o = slice(32 * t - 32, 32 * t)
+        x = V(ts, [dep], T.pa[:, o], T.pt[:, o], float(2048 - P * d), None, A.add)
+        x = V(ts, [x], T.np[:, o], T.pa[:, o], 2047, None, A.bitwise_and)
+        of = V(tc, [x], T.of[:, o], T.np[:, o])
+        x = places((x, T.np[:, o]), T.lo[:, o], T.hb[:, o], T.tl[:, o], T.hm[:, o], T.po[:, o])()
+        return of, V(tc, [x], T.op[:, o], T.po[:, o])
+
+    def row(t, of):
+        return S([gi, io, of], T["nr%d" % t][:], T.iot[:].indirect(T.of[:, 32 * t - 32:32 * t]), F.Copy, scale=U)
+
+    def deltas(t, nr):
+        r, v = T["nr%d" % t], T["vd%d" % t]
+        z = V(tt, [nr], v[:, 0:511], r[:, 0:511], r[:, 1:512], A.subtract)
+        return V(tc, [z], v[:, 3:512:4], r[:, 3:512:4])
+
+    nr, vd, fl0, ops = {}, {}, {}, {}
+    of1, ops[1] = listed(1, p1)
+    nr[1] = row(1, of1)
+    ic, fc = T.ic, T.fc
+    b1 = V(ts, [gp], ic[:, 1:2], ic[:, 0:1], 7, None, A.bitwise_and)
+    b4 = V(ts, [gp], ic[:, 4:5], ic[:, 0:1], 3, None, A.logical_shift_right)
+    b5 = V(ts, [gp], ic[:, 5:6], ic[:, 0:1], 15, None, A.bitwise_and)
+    b2 = V(ts, [b1], ic[:, 2:3], ic[:, 1:2], float(N - d), None, A.add)
+    b3 = V(ts, [b2], ic[:, 3:4], ic[:, 2:3], 7, None, A.bitwise_and)
+    fl0[1] = V(ms, [], T.fl1[:, 0:512:4], 0.0)
+    b6 = V(tc, [b3, b4, b5], fc[:, 0:3], ic[:, 3:6])
+    rh = V(tc, [gij], T.rh[:], T.ij[:])
+    c1 = V(ts, [b6], fc[:, 3:4], fc[:, 0:1], -256.0 * U, -127.5 * U, A.mult, A.add)
+    c2 = V(ts, [b6], fc[:, 4:5], fc[:, 0:1], 0.0, -100.0, A.is_equal, A.mult)
+    c4 = V(ts, [b6], fc[:, 10:11], fc[:, 0:1], 0.0, None, A.is_equal)
+    dup = V(ts, [b6, giy], T.dup[:], T.iy[:], fc[:, 2:3], None, A.add)
+    nbc = V(tt, [c1, c2], fc[:, 5:6], fc[:, 3:4], fc[:, 4:5], A.add)
+    nq = S([nr[1], c4], T.nq[:], T.nr1[:, 0:512:4], F.Copy, scale=fc[:, 10:11])
+    r2 = V(ms, [], T.rsb[:, 0:256], BIG)
+    sb0 = V(ms, [], T.sb[:], 0.0)
+    rsb = V(ms, [r2], T.rsb[:, 0:256:16], -BIG)
+    qa = V(qz, [da], T.aq[:], T.aqs[:], T.at[:])
+    vd[1] = deltas(1, nr[1])
+
+    def spread(land, deps, sems):
+        for k in range(8):
+            D("ys"[k % 2], deps, sems[k % 2], T.sc[16 * k:16 * k + 1, :], land[:])
+        return [(n, total[n]) for n in sems]
+
+    def choose(t, deps):
+        ga_, mx_, fl_, cn_ = T["ga%d" % t], T["mx%d" % t], T["fl%d" % t], T["cn%d" % t]
+        deps = deps + [ops[t]]
+        x1 = V(tc, deps, ga_[:, 0:256], T.sc[:].indirect(T.op[:, 32 * t - 32:32 * t - 16]))
+        x2 = S(deps, ga_[:, 256:512], T.sc[:].indirect(T.op[:, 32 * t - 16:32 * t]), F.Copy)
+        m = V(scan, [x1, x2, rs], mx_[:], T.rs[:], ga_[:], -BIG, A.min, A.max)
+        for k in (1, 2, 3):
+            f = V(tt, [m, fl0[t]], fl_[:, k:512:4], ga_[:, k:512:4], mx_[:, k - 1:512:4], A.is_le)
+        return V(scan, [f, vd[t]], cn_[:], fl_[:], T["vd%d" % t][:], 0.0, A.mult, A.add), x1, x2
+
+    def whole(t, n, lists, out, deps):
+        cc, cct, cx, cn = T["cc%d" % t], T["cct%d" % t], T["cx%d" % t], T["cn%d" % t]
+        w, k = n // 2, lists.shape[1] // 2
+        x = V(tc, deps, cc[:], cn[:, 3:512:4])
+        x = V(tp, [x], cct[:], cc[:])
+        x1 = V(tc, [x], cx[:, 0:w], cct[:].indirect(lists[:, 0:k]))
+        x2 = S([x], cx[:, w:n], cct[:].indirect(lists[:, k:2 * k]), F.Copy)
+        return V(tp, [x1, x2], out, cx[:])
+
+    def keep1(c, deps):
+        x = S(deps + [nbc], T.ad1[:, 0:128], c, F.Abs, bias=fc[:, 5:6])
+        mk = V(ts, [x], T.mk1[:, 0:128], T.ad1[:, 0:128], 128.0 * U, None, A.is_lt)
+        x = V(scan, [mk, zr], T.ct1[:, 0:128], T.mk1[:, 0:128], T.zer[:, 0:128], 0.0, A.add, A.add)
+        y = V(tt, [mk] + deps, T.mc[:], T.mk1[:, 0:128], c, A.mult)
+        x = V(tp, [x], T.ta[:], T.ct1[:, 96:128])
+        y = V(tt, [y, nq], T.mn[:], T.mc[:], T.nq[:], A.add)
+        y = S([y, dup], T.exm[:], T.mn[:].indirect(T.dup[:, 0:16]), F.Copy)
+        x = V(tc, [x, sb0], T.sb[:, 16:32], T.ta[:, 0:16])
+        x = V(tp, [x], T.tb[:], T.sb[:])
+        x = V(ts, [x], T.k2[:], T.ct1[:, 0:128], T.tb[:, 31:32], float(CAP), A.add, A.is_le)
+        return V(tt, [x, y], T.ex1[:, 0:256], T.k2[:].indirect(T.dup[:, 0:16]), T.exm[:], A.mult)
+
+    def onto(t, deps):
+        w = P * t
+        x = V(tp, deps, T["tr%d" % t][:, 0:w], T["ex%d" % t][:, 0:w])
+        return V(scan, [x, rsb], T["mr%d" % t][:, 0:w], T.rsb[:, 0:w], T["tr%d" % t][:, 0:w], -BIG, A.min, A.max)
+
+    def states(x, xs, banks, et, h, tm, q, qs, edep, picks, between=None):
+        m, s, out = {}, {}, []
+        for k in (0, 1):
+            for i in range(4):
+                m[k, i] = MM(picks[k] + [qa], banks[k][:, 512 * i:512 * i + HALF], T.aq[:, 128 * i:128 * i + 128], T.aqs[:, 128 * i:128 * i + 128],
+                             x[:, HALF * k:HALF * k + HALF], xs[:, HALF * k:HALF * k + HALF])
+        for k in (0, 1):
+            for i in range(4):
+                o = P * i + HALF * k
+                s[k, i] = S([m[k, i]], tm[:, o:o + HALF], banks[k][:, 512 * i:512 * i + HALF], F.Copy, scale=0.05)
+            if k == 0 and between is not None:
+                between()
+        for k in (0, 1):
+            for i in range(4):
+                o = P * i + HALF * k
+                c = slice(4 * HALF * k + i, 4 * HALF * (k + 1), 4)
+                a = V(tt, [s[k, i], edep], h[:, c], tm[:, o:o + HALF], et[:, c], A.add)
+            out.append(V(qz, [a], q[:, HALF * k:HALF * k + HALF], qs[:, HALF * k:HALF * k + HALF], h[:, 4 * HALF * k:4 * HALF * (k + 1)]))
+        return out
+
+    got = spread(T.sld1, [og, ("r0", 7 * neng), c0, sc0], ("ds0", "ds1"))
+    e1 = D("y", got, "de1", T.e1t[:], T.e1[:, :])
+    for k in range(8):
+        p2 = D("y", [], "dp2", T.pt[16 * k:16 * k + 16, 32:64], T.p2[:, 32 * (k % 2):32 * (k % 2) + 32])
+    e2 = D("y", [], "de2", T.e2t[:], T.e2[:, :])
+    dw = D("y", [], "dw", T.wt[:], T.w[:, :])
+    ch, g0v, g0s = choose(1, got)
+    cr = whole(1, 128, T.rh, T.cr1[:], [ch, rh])
+    z = onto(1, [keep1(T.cr1[:], [cr])])
+    o1 = V(ts, [z], T.ofx1[:, 0:8], T.mr1[:, 7:256:32], 4096.0, None, A.mult)
+    o2 = V(ts, [z], T.ofx1[:, 8:16], T.mr1[:, 23:256:32], 4096.0, None, A.mult)
+    arr = [("h%d" % i, (PIECES + 1) * neng) for i in others]
+    tj = T.tj
+    ji = V(tc, [o2], tj[:, 0:16], T.ofx1[:])
+    rest = places((ji, tj[:, 0:16]), tj[:, 16:32], tj[:, 32:48], tj[:, 48:64], tj[:, 64:80], tj[:, 80:96])
+
+    def pick(x, xs, w, ws, o, k, deps):
+        c = slice(HALF * k, HALF * k + HALF)
+        a = V(tc, deps, x[:, c].bitcast(u32), w.bitcast(u32).indirect(o[:, 8 * k:8 * k + 8]))
+        return [a, S(deps, xs[:, c], ws.indirect(o[:, 8 * k:8 * k + 8]), F.Copy)]
+
+    picks = [pick(T.x1, T.x1s, T.hw[:], T.hws[:], T.ofx1, k, [o1, o2] + arr) for k in (0, 1)]
+    os1 = V(tc, [rest()], T.ofs1[:], tj[:, 80:96])
+    srs = []
+
+    def chosen_scores():
+        srs.append(S([os1], T.scr1[:], T.sc[:].indirect(T.ofs1[:]), F.Copy))
+        for k in (0, 1):
+            srs.append(D("y", [srs[0]], "dsc", T.scc[:, k:k + 1], T.scr1[0:1, HALF * k:HALF * k + HALF]))
+
+    q1 = states(T.x1, T.x1s, (T.pr, T.ps), T.e1t, T.h1, T.tm1, T.hq, T.hqs, e1, picks, chosen_scores)
+    for k in (0, 1):
+        mg = scores([q1[k]], T.hq[:, HALF * k:HALF * k + HALF], T.hqs[:, HALF * k:HALF * k + HALF], T.pr[:, 512 * k:512 * k + 128])
+    g1 = V(tt, [mg, srs[2]], T.g1c[:], T.pr[:, 0:1024:512], T.scc[:], A.add)
+
+    send([g1], "rg", T.g1c[:], all_, [T.sld2[rel(d, i)] for i in others])
+    og = D("y", [g1], "dog1", T.sld2[0], T.g1c[:])
+    of2, ops[2] = listed(2, p2)
+    nr[2] = row(2, of2)
+    dup4 = V(ts, [b6, giy], T.dup4[:], T.iy[:], fc[:, 2:3], 4.0, A.add, A.mult)
+    fl0[2] = V(ms, [], T.fl2[:, 0:512:4], 0.0)
+    i5c = V(ts, [b6], fc[:, 6:7], fc[:, 0:1], 512.0, None, A.mult)
+    c3 = V(ts, [b6], fc[:, 7:8], fc[:, 0:1], 512.0 + 256.0 * U, 1.0, A.mult, A.add)
+    rj = V(tc, [giz], T.rj[:], T.iz[:])
+    t0c = V(tt, [c3], fc[:, 8:9], fc[:, 7:8], fc[:, 1:2], A.add)
+    r2 = V(ms, [], T.rsb[:, 256:512], BIG)
+    t1c = V(ts, [t0c], fc[:, 9:10], fc[:, 8:9], -1.0, -16.0, A.mult, A.add)
+    cz = V(ms, [], T.cr2[:, 0:32], 0.0)
+    vd[2] = deltas(2, nr[2])
+    z = S([nr[2], dup4], T.nx2[:], T.nr2[:].indirect(T.dup4[:, 0:16]), F.Copy)
+    z = V(tp, [z], T.nt2[:], T.nx2[:])
+    rsb = V(ms, [r2], T.rsb[:, 256:512:16], -BIG)
+    n0 = V(ts, [z], T.ti[:, 0:8], T.nt2[:, 0:256:32], 4096.0, None, A.mult)
+    n0 = V(ts, [z], T.ti[:, 8:16], T.nt2[:, 16:256:32], 4096.0, None, A.mult)
+    q1b = V(qz, q1, T.w2[:, 0:P], T.w2s[:, 0:P], T.h1[:])
+    qw = V(qz, [dw], T.wq[:], T.wqs[:], T.wt[:])
+    got = spread(T.sld2, [og, ("rg", 7 * neng), g0v, g0s, srs[0]], ("ds2", "ds3"))
+
+    ch = choose(2, got)[0]
+    cr_ = T.cr2[:, 32:288]
+    cr = whole(2, 256, T.rj, cr_, [ch, rj])
+    x = S([cr, nbc], T.ad2[:], cr_, F.Abs, bias=fc[:, 5:6])
+    y = V(tt, [cr, cz], T.dc[:], cr_, T.cr2[:, 31:287], A.subtract)
+    mk = V(ts, [x], T.mk2[:], T.ad2[:], 128.0 * U, None, A.is_lt)
+    z = V(scan, [mk, y, i5c], T.ct2[:], T.mk2[:], T.dc[:], fc[:, 6:7], A.add, A.add)
+    zz = V(tt, [z], T.zz2[:], T.mk2[:], T.ct2[:], A.mult)
+    y1 = S([zz, t1c], T.d1[:], T.zz2[:], F.Identity, bias=fc[:, 9:10])
+    y0 = V(ts, [zz, t0c], T.d0[:], T.zz2[:], fc[:, 8:9], None, A.subtract)
+    y0 = V(red, [y0], T.rv[:, 0:1], T.d0[:], AxisListType.X, A.min, apply_absolute_value=True)
+    y1 = V(red, [y1], T.rv[:, 1:2], T.d1[:], AxisListType.X, A.min, apply_absolute_value=True)
+    rq = V(ts, [y0, y1], T.rq[:], T.rv[:], 255.0 * U, 4096.0, A.min, A.mult)
+    send([rq], "rr", T.rq[:], all_, [T.rqs[:, 2 * rel(d, i):2 * rel(d, i) + 2] for i in others])
+    for k in range(8):
+        D("ys"[k % 2], [("rr", 7 * neng)], ("dofq", "dofs")[k % 2], T.ofq[16 * k:16 * k + 16, 2:16], T.rqs[d:128:8, 2:16])
+    oq = [("dofq", 64), ("dofs", 64)]
+    z = V(tc, [zz, dup], T.ex2[:], T.zz2[:].indirect(T.dup[:]))
+    z = onto(2, [z])
+    ti = T.ti
+    zi = V(ts, [z], ti[:, 16:32], T.mr2[:, 7:512:32], 4096.0, None, A.mult)
+    ky = V(ts, [zi], ti[:, 48:64], ti[:, 16:32], 12, 511, A.logical_shift_right, A.bitwise_and)
+    ci = V(ts, [zi], ti[:, 32:48], ti[:, 16:32], 4095, None, A.bitwise_and)
+    kq = V(ts, [zi], ti[:, 112:128], ti[:, 16:32], 21, None, A.logical_shift_right)
+    kf = V(ts, [ky], ti[:, 64:80], ti[:, 48:64], float(CAP), None, A.is_le)
+    pc = V(tc, oq + q1, T.sp[:].bitcast(u32), T.hq[:].bitcast(u32).indirect(T.ofq[:, 2:16]))
+    pk = S(oq + q1, T.sps[:], T.hqs[:].indirect(T.ofq[:, 2:16]), F.Copy)
+    ca, cb = [], []
+    for i in others:
+        a, b = CAP * (rel(i, d) - 1), P + CAP * (rel(d, i) - 1)
+        ca.append((T.sp[:, a:a + CAP].bitcast(u8), T.w2[:, b:b + CAP].bitcast(u8)))
+        cb.append((T.sps[:, a:a + CAP], T.w2s[:, b:b + CAP]))
+    send_each([pc], "rc", ca)
+    send_each([pk], "rc", cb)
+    kc = V(tt, [kf, ci], ti[:, 80:96], ti[:, 64:80], ti[:, 32:48], A.mult)
+    x = V(ts, [kq], ti[:, 128:144], ti[:, 112:128], 32.0, None, A.mult)
+    cf = V(tt, [kc, n0], ti[:, 96:112], ti[:, 80:96], ti[:, 0:16], A.max)
+    x = V(tt, [x, ky], ti[:, 144:160], ti[:, 128:144], ti[:, 48:64], A.add)
+    x = V(tt, [x, kf], ti[:, 160:176], ti[:, 144:160], ti[:, 64:80], A.mult)
+    y = V(ts, [x], ti[:, 176:192], ti[:, 160:176], 0.0, 223.0, A.is_gt, A.mult)
+    x = V(tt, [y], ti[:, 192:208], ti[:, 160:176], ti[:, 176:192], A.add)
+    x = V(tt, [x], ti[:, 208:224], ti[:, 192:208], ti[:, 0:16], A.max)
+    ox2 = V(tc, [x], T.ofx2[:], ti[:, 208:224])
+    jp = places((cf, ti[:, 96:112]), ti[:, 224:240], ti[:, 240:256], tj[:, 96:112], tj[:, 112:128], tj[:, 128:144])()
+    os2 = V(tc, [jp], T.ofs2[:], tj[:, 128:144])
+
+    def absolute(x, n, a, b, out):
+        x = V(ts, [x], a, n, float(P * d), None, A.add)
+        x = V(ts, [x], b, a, 2047, None, A.bitwise_and)
+        return V(tc, [x], out, b)
+
+    oa1 = absolute(ji, tj[:, 0:16], tj[:, 144:160], tj[:, 160:176], T.ofa1[:])
+    oa2 = absolute(cf, ti[:, 96:112], tj[:, 176:192], tj[:, 192:208], T.ofa2[:])
+    sr2 = S([os2], T.scr2[:], T.sc[:].indirect(T.ofs2[:]), F.Copy)
+    c1r = S([oa1, gi, io], T.chr1[:], T.iot[:].indirect(T.ofa1[:]), F.Copy)
+    c2r = S([oa2], T.chr2[:], T.iot[:].indirect(T.ofa2[:]), F.Copy)
+    D("s", [c1r], "dch", T.ch[0:1, :], T.chr1[0:1, :])
+    D("s", [c2r], "dch", T.ch[1:2, :], T.chr2[0:1, :])
+
+    picks = [pick(T.x2, T.x2s, T.w2[:, 0:480], T.w2s[:, 0:480], T.ofx2, k, [("rc", 14), ox2, q1b]) for k in (0, 1)]
+    q2 = states(T.x2, T.x2s, (T.ps, T.pr), T.e2t, T.h2, T.tm2, T.zq, T.zqs, e2, [p + [g1] for p in picks])
+    for k in (0, 1):
+        c = slice(HALF * k, HALF * k + HALF)
+        m1 = MM([q2[k], qw], T.ps[:, 512 * k:512 * k + HALF], T.wq[:], T.wqs[:], T.zq[:, c], T.zqs[:, c])
+        m2 = MM([q2[k]], T.ps[:, 1024 + 512 * k:1024 + 512 * k + HALF], T.uq[:], T.uqs[:], T.zq[:, c], T.zqs[:, c])
+        D("y", [q2[k]], "dout", T.oc[:, 4 * HALF * k:4 * HALF * (k + 1)], T.zq[:, c].bitcast(u8))
+        yy = S([m1], T.ys[:, c], T.ps[:, 512 * k:512 * k + HALF], F.Copy)
+        gg = V(tt, [m2, sr2], T.go[0:1, c], T.ps[0:1, 1024 + 512 * k:1024 + 512 * k + HALF], T.scr2[0:1, c], A.add)
+        if k:
+            for i in range(4):
+                D("y", [q2[k]], "dout", T.osc[4 * i:4 * i + 4, :], T.zqs[32 * i:32 * i + 4, :])
+        D("y" if k == 0 else "s", [yy], ("dout", "dch")[k], T.y[:, c], T.ys[:, c])
+    D("s", [gg], "dch", T.g[0:1, :], T.go[0:1, :])
+
+    wait("g", [(n, total[n]) for n in total])

@@ -3,33 +3,35 @@ from concourse.mybir import dt, AluOpType as A, AxisListType, ActivationFunction
 
 N, P, CAP = 8, 256, 32
 HALF = P // 2
-PIECES = 2
+OWN = P * (N - 1)
 BIG = 9e29
 U = 1.0 / 4096.0
+GAP = 2.0 ** 18
+MAGIC = 2.0 ** 41
+B0 = 8
 
 _f32, _i32, _u16, _bf = "float32", "int32", "uint16", "bfloat16"
 SCRATCH = {"ps": ("psum", [128, 2048], _f32), "pr": ("psum", [128, 2048], _f32), "sld1": ("dram", [8, 128, 2], _f32), "sld2": ("dram", [8, 128, 2], _f32)}
 for _d, _l in (
-        (_bf, "e0t 1024 e1t 1024 e2t 1024 ut 512 at 2048 wt 512 h1 1024 h2 1024"),
-        (_f32, "tm1 1024 tm2 1024 sc 2048 iot 2048 rs 512 rsb 512 zer 256 ta 32 sb 32 tb 32 nq 128 cc1 128 cct1 128 cx1 128 cr1 128 "
-               "cc2 128 cct2 128 cx2 256 cr2 288 fc 16 d0 256 d1 256 rv 2 scr1 256 scr2 256 scc 2 g0c 2 g1c 2 chr1 256 chr2 256 go 256 ys 256 "
-               "mc 128 mn 128 exm 256 k2 128 nx2 256 nt2 256 dc 256 zz2 256"),
-        (_i32, "pt 64 pa 64 np 64 lo 64 hb 64 tl 64 hm 64 po 64 iz 16 ij 8 ic 8 iy 32 ti 256 tj 256"),
-        (_u16, "of 64 op 64 rj 16 rh 8 dup 32 dup4 32 rq 2 rqs 16 ofq 16 ofx1 16 ofs1 16 ofa1 16 ofx2 16 ofs2 16 ofa2 16")):
+        (_bf, "e0t 1024 e1t 1024 e2t 1024 ut 512 at 2048 wt 512 h1 1024 h2 1024 zer 256 mk1 256 mk2 256 ct1 256 ct2 256 cq2 256"),
+        (_f32, "tm1 1024 tm2 1024 sc 2048 rs 32 rsb 256 fc 16 s2 256 t1 128 t2 128 nt 128 dl 128 vd 64 xw 128 zz 256 z2 256 b2 256 rv 2 "
+               "scr1 256 scr2 256 scc 2 g0c 2 g1c 2 go 256 ys 256 cf 32 cht 32"),
+        (_i32, "pt 144 pa 128 np 128 lo 128 hb 128 wq2 128 tl 128 wg 128 ic 8 iy 16 ix 16 ti 256 tj 256"),
+        (_u16, "op 64 l1 16 dup 16 rq 2 rqs 16 ofq 16 ofx1 16 ofs1 16 ofx2 16 ofs2 16")):
     _w = _l.split()
     for _k in range(0, len(_w), 2):
         SCRATCH[_w[_k]] = ("sbuf", [128, int(_w[_k + 1])], _d)
-for _n, _c in (("uq", 128), ("aq", 512), ("wq", 128), ("hw", 2048), ("hr", 256), ("x1", 256), ("hq", 256), ("sp", 224), ("w2", 512), ("x2", 256),
+for _n, _c in (("uq", 128), ("aq", 512), ("wq", 128), ("hw", 2048), ("hr", 128), ("x1", 256), ("hq", 256), ("sp", 224), ("w2", 512), ("x2", 256),
                ("zq", 256)):
     SCRATCH[_n] = ("sbuf", [128, _c], "float8_e4m3fn_x4")
     SCRATCH[_n + "s"] = ("sbuf", [128, _c], "uint8")
+SCRATCH["hs"] = ("sbuf", [128, 224], "uint8")
 for _t in ("1", "2"):
-    for _n, _c in (("ga", 512), ("mx", 512), ("fl", 512), ("cn", 512), ("nr", 512), ("vd", 512),
-                   ("ad", 256), ("mk", 256), ("ct", 256), ("ex", 512), ("tr", 512), ("mr", 512)):
+    for _n, _c in (("ga", 512), ("tg", 544), ("mx", 32), ("fl", 32), ("xd", 256), ("xr", 256), ("bd", 256), ("yy", 256), ("yt", 256), ("mr", 256)):
         SCRATCH[_n + _t] = ("sbuf", [128, _c], _f32)
 
-SEMAPHORES = ["cv", "cs", "ct", "cg", "l0", "ls", "r0", "rg", "rr", "rc", "hk"] + ["h%d" % i for i in range(N)] + ["hc%d" % i for i in range(PIECES)]
-SEMAPHORES += ["de0", "du", "dp1", "dp2", "da", "de1", "dw", "de2", "dog0", "dog1", "ds0", "ds1", "ds2", "ds3", "dsc", "dofq", "dofs", "dch", "dout"]
+SEMAPHORES = ["cv", "cs", "ct", "cg", "l0", "ls", "r0", "rg", "rr", "rc", "hh", "hc", "hk", "hz"]
+SEMAPHORES += ["de0", "de0b", "du", "dp1", "dp2", "da", "de1", "dw", "de2", "dog0", "dog1", "ds0", "ds1", "ds2", "ds3", "dsc", "dofq", "dofs", "dch", "dout"]
 
 
 def bits(m):
@@ -39,30 +41,18 @@ def bits(m):
 def plan(d, cores, topo):
     me = cores[d]
     here = topo.chip(me)
-    order = sorted([i for i in range(N) if i != d], key=lambda i: (-min((i - d) % N, (d - i) % N), (i - d) % N))
+    order = [(d + k) % N for k in range(1, N)]
     mate = [i for i in order if topo.mates(here, topo.chip(cores[i]))]
     plane = [i for i in order if topo.same_plane(here, topo.chip(cores[i]))]
     far = [i for i in order if i not in mate + plane]
     used, out = [me], []
-    for same, ranks in ((True, far[2:] + mate), (True, plane[1:]), (False, far[:1] + plane[:1]), (False, far[1:2])):
-        able = [h for h in topo.cores_of(me) if h not in used and (topo.die(h) == topo.die(me)) == same and all(topo.may_write(h, cores[i]) for i in ranks)]
+    for half, ranks, asked in ((0, far, order[:4]), (0, plane, []), (1, far, order[4:]), (1, plane, [])):
+        able = [h for h in topo.cores_of(me) if h not in used and (topo.die(h) == topo.die(me)) == (half == 0)
+                and all(topo.may_write(h, cores[i]) for i in ranks + asked)]
         able.sort(key=lambda h: sum(topo.may_write(h, cores[i]) for i in order))
         used.append(able[0])
-        out.append((able[0], ranks))
-    return [(h, r, out[k + 1][0] if k % 2 == 0 else None) for k, (h, r) in enumerate(out)]
-
-
-def chip_engines(topo, core, near, far):
-    return topo.mask(core, near) & ~topo.mask(core, far)
-
-
-def pieces(T):
-    w = P // PIECES
-    out = []
-    for k in range(PIECES):
-        out.append(("hc%d" % k, T.hr[:, w * k:w * k + w].bitcast(dt.uint8), lambda q, k=k: T.hw[:, P * q + w * k:P * q + w * k + w].bitcast(dt.uint8)))
-    out.append(("hk", T.hrs[:], lambda q: T.hws[:, P * q:P * q + P]))
-    return out
+        out.append((able[0], half, ranks, asked))
+    return mate, out
 
 
 def dst_of(topo, c):
@@ -70,25 +60,44 @@ def dst_of(topo, c):
     return DstId(rid=rid, pnc=pid)
 
 
+def rel(s, r):
+    return (s - r - 1) % N
+
+
+def mask_of(es):
+    return sum(1 << e for e in es)
+
+
+def feed_engines(topo, core, near, far):
+    out = topo.engines(core, far)
+    return out, [e for e in topo.engines(core, near) if e not in out]
+
+
 def hand_on(g, core, T, topo):
+    u8 = dt.uint8
     for d in range(N):
-        for h, ranks, sub in plan(d, T.cores, topo):
+        for h, half, ranks, asked in plan(d, T.cores, topo)[1]:
             if h != core:
                 continue
-            far = T.cores[ranks[0]]
-            mask = topo.mask(core, far)
-            came = bits(chip_engines(topo, T.cores[d], core, far))
+            outer, inner = feed_engines(topo, T.cores[d], core, T.cores[ranks[0]])
+            es = topo.engines(core, T.cores[ranks[0]])
             n = 0
-            for sem, here, land in pieces(T):
+            at = [P * rel(d, i) + HALF * half for i in ranks]
+            for sem, came, here, lands in (("hc", len(inner), T.hr[:].bitcast(u8), [T.hw[:, a:a + HALF].bitcast(u8) for a in at]),
+                                           ("hk", len(inner) // 2, T.hrs[:], [T.hws[:, a:a + HALF] for a in at])):
                 g.wait_ge(T.sem[sem], came)
-                ts = [RemoteDMATransfer(dst_ids=[dst_of(topo, T.cores[i]) for i in ranks], dma_engine_mask=mask, remote_sem=T.sem["h%d" % d], srcs=[here],
-                                        dsts=[land((d - i) % N) for i in ranks])]
-                n += bits(mask)
-                if sub is not None:
-                    m = chip_engines(topo, core, sub, far)
-                    ts.insert(0, RemoteDMATransfer(dst_ids=[dst_of(topo, sub)], dma_engine_mask=m, remote_sem=T.sem[sem], srcs=[here], dsts=[here]))
-                    n += bits(m)
+                g.remote_dma_fused([RemoteDMATransfer(dst_ids=[dst_of(topo, T.cores[i]) for i in ranks], dma_engine_mask=mask_of(es), remote_sem=T.sem.hh,
+                                                      srcs=[here], dsts=lands)], local_sem=T.sem.ls)
+                n += len(es)
+            if asked:
+                g.wait_ge(T.sem.hz, len(inner))
+                ts = []
+                for k, i in enumerate(asked):
+                    a, b = CAP * rel(i, d), CAP * rel(d, i)
+                    ts.append(RemoteDMATransfer(dst_ids=[dst_of(topo, T.cores[i])], dma_engine_mask=mask_of(es[2 * k:2 * k + 2]), remote_sem=T.sem.rc,
+                                                srcs=[T.hs[:, a:a + CAP]], dsts=[T.w2s[:, b:b + CAP]]))
                 g.remote_dma_fused(ts, local_sem=T.sem.ls)
+                n += 2 * len(asked)
             g.wait_ge(T.sem.ls, n)
 
 
@@ -141,118 +150,120 @@ def rank_program(g, core, T, topo):
 
     others = [(d + k) % N for k in range(1, N)]
     all_ = [cores[i] for i in others]
-    mask = topo.mask(core, all_[0])
-    for c in all_:
-        mask &= topo.mask(core, c)
-    engs = [e for e in topo.engines(core, all_[0]) if mask >> e & 1]
+    mate, helpers = plan(d, cores, topo)
+    engs, inner = feed_engines(topo, core, helpers[0][0], all_[0])
     neng = len(engs)
-    helpers = [h for h, r, sub in plan(d, cores, topo)][0::2]
-    inner = chip_engines(topo, core, helpers[0], all_[0])
 
-    def sent(name, n):
-        total[name] = total.get(name, 0) + n
-        return (name, total[name])
-
-    def send(deps, sem, src, to, dsts, local="ls", m=mask):
+    def call(deps, transfers, local="ls"):
         wait("g", deps)
-        g.remote_dma_fused([RemoteDMATransfer(dst_ids=[dst_of(topo, c) for c in to], dma_engine_mask=m, remote_sem=T.sem[sem], srcs=[src], dsts=dsts)],
-                           local_sem=T.sem[local])
-        return sent(local, bits(m))
+        g.remote_dma_fused([RemoteDMATransfer(dst_ids=[dst_of(topo, c) for c in to], dma_engine_mask=mask_of(es), remote_sem=T.sem[sem], srcs=[src], dsts=dsts)
+                            for sem, es, src, to, dsts in transfers], local_sem=T.sem[local])
+        total[local] = total.get(local, 0) + sum(len(t[1]) for t in transfers)
+        return (local, total[local])
 
-    def send_each(deps, sem, pairs):
-        wait("g", deps)
-        g.remote_dma_fused([RemoteDMATransfer(dst_ids=[dst_of(topo, all_[k])], dma_engine_mask=1 << engs[k], remote_sem=T.sem[sem], srcs=[a], dsts=[b])
-                            for k, (a, b) in enumerate(pairs)], local_sem=T.sem.ls)
-        return sent("ls", len(pairs))
-
-    def rel(s, r):
-        return (s - r) % N
-
-    e0 = D("y", [], "de0", T.e0t[:], T.e0[:, :])
-    uu = D("s", [], "du", T.ut[:], T.u[:, :])
+    e0 = [D("y", [], "de0", T.e0t[:, 0:512], T.e0[:, 0:512])]
+    uu = D("s", [], "du", T.ut[:, 0:8], T.u[:, 0:8])
+    e0.append(D("y", [], "de0b", T.e0t[:, 512:1024], T.e0[:, 512:1024]))
     for k in range(8):
-        p1 = D("y", [], "dp1", T.pt[16 * k:16 * k + 16, 0:32], T.p1[:, 32 * (k % 2):32 * (k % 2) + 32])
+        b = B0 - k % 2
+        p1 = D("y", [], "dp1", T.pt[16 * k:16 * k + 16, b:b + 64], T.p1[:, :])
+        p2 = D("s", [], "dp2", T.pt[16 * k:16 * k + 16, b + 64:b + 128], T.p2[:, :])
     da = D("y", [], "da", T.at[:], T.a[:, :])
 
-    gi = G(g.iota, [], T.iot[:, 0:512], [[1, 512]], 0, 0, allow_small_or_imprecise_dtypes=True)
-    gp = G(g.iota, [], T.ic[:, 0:1], [[0, 1]], 0, 1)
-    giy = G(g.iota, [], T.iy[:], [[16, 16], [0, 2]], 0, 0)
-    giz = G(g.iota, [], T.iz[:], [[16, 2], [32, 4], [0, 2]], 0, 0)
-    gij = G(g.iota, [], T.ij[:], [[16, 8]], 0, 0)
+    gp = G(g.iota, [], T.ic[:, 0:2], [[N - 1 - d, 2]], 0, 1)
+    giy = G(g.iota, [], T.iy[:], [[32, 8], [0, 2]], 0, 0)
+    gix = G(g.iota, [], T.ix[:], [[4, 8], [0, 2]], 3, 0)
+    ic, fc = T.ic, T.fc
     c0 = V(ms, [], T.sc[:, 0:512], 0.0)
-    zr = V(ms, [], T.zer[:], 0.0)
-    r1 = V(ms, [], T.rs[:], BIG)
+    uz = V(ms, [], T.ut[:, 8:512], 0.0)
+    b3 = V(ts, [gp], ic[:, 2:3], ic[:, 1:2], 7, None, A.bitwise_and)
+    b5 = V(ts, [gp], ic[:, 4:5], ic[:, 0:1], 31, None, A.bitwise_and)
+    b4 = V(ts, [gp], ic[:, 3:4], ic[:, 0:1], 3, None, A.logical_shift_right)
+    b6 = V(tc, [b3, b4, b5], fc[:, 0:3], ic[:, 2:5])
     for k in (1, 2, 3):
-        sc0 = S([c0], T.sc[:, 512 * k:512 * k + 512], T.sc[:, 0:512], F.Copy)
-    for k in (1, 2, 3):
-        io = S([gi], T.iot[:, 512 * k:512 * k + 512], T.iot[:, 0:512], F.Identity, bias=512.0 * k)
-    rs = V(ms, [r1], T.rs[:, 0:512:4], -BIG)
+        S([c0], T.sc[:, 512 * k:512 * k + 512], T.sc[:, 0:512], F.Copy)
 
-    q0 = V(qz, [e0], T.hw[:, 0:P], T.hws[:, 0:P], T.e0t[:])
-    quq = V(qz, [uu], T.uq[:], T.uqs[:], T.ut[:])
+    def fill(deps, out, value):
+        return S(deps + [c0], out, T.sc[:, 0:out.shape[1]], F.Identity, bias=value)
+
+    def col(deps, k, j, scale, bias, func=F.Identity):
+        return S(deps, fc[:, k:k + 1], fc[:, j:j + 1], func, scale=scale, bias=bias)
+
+    r1 = fill([], T.rs[:], BIG)
+    r2 = fill([], T.rsb[:], -BIG)
+    c4 = col([b6], 3, 0, 1.0, -6.0, F.Relu)
+    c1 = col([b6], 5, 0, -GAP * U, 0.0)
+    xz = fill([], T.xw[:], 0.0)
+    rs = fill([r1], T.rs[:, 0:32:4], -BIG)
+    c5 = col([c4], 9, 3, 64.0, 0.0)
+    rsb = fill([r2], T.rsb[:, 0:256:16], BIG)
+    zr = fill([], T.zer[:], 0.0)
+    cm = col([b6], 4, 0, GAP, MAGIC)
+    nb = col([c4, c1], 6, 3, 7 * GAP * U, fc[:, 5:6])
+    t0 = [fill([], T["tg%d" % t][:, 0:32], 0.0) for t in (1, 2)]
+    c2 = col([b6], 7, 0, -(GAP + P) * U, 0.0)
+    c3 = col([b6], 8, 1, -1.0, -1.0)
+    c6 = col([c4], 10, 3, CAP + 0.5, -float(CAP))
 
     def scores(deps, w, ws, ps):
-        return MM(deps + [quq], ps, w, ws, T.uq[:], T.uqs[:])
+        return MM(deps, ps, w, ws, T.uq[:], T.uqs[:])
 
+    hc = [slice(OWN + HALF * k, OWN + HALF * k + HALF) for k in (0, 1)]
+    q0 = [V(qz, [e0[0]], T.hw[:, hc[0]], T.hws[:, hc[0]], T.e0t[:, 0:512])]
+    quq = V(qz, [uu, uz], T.uq[:], T.uqs[:], T.ut[:])
+    q0.append(V(qz, [e0[1]], T.hw[:, hc[1]], T.hws[:, hc[1]], T.e0t[:, 512:1024]))
     for k in (0, 1):
-        m = scores([q0], T.hw[:, HALF * k:HALF * k + HALF], T.hws[:, HALF * k:HALF * k + HALF], T.ps[:, 512 * k:512 * k + 128])
+        m = scores([q0[k], quq], T.hw[:, hc[k]], T.hws[:, hc[k]], T.ps[:, 512 * k:512 * k + 128])
     g0 = V(tc, [m], T.g0c[:], T.ps[:, 0:1024:512])
-    parts = pieces(T)
-    send([q0], parts[0][0], parts[0][2](0), helpers, [parts[0][1]] * 2, "l0", inner)
-    send([g0], "r0", T.g0c[:], all_, [T.sld1[rel(d, i)] for i in others])
-    for sem, there, here in parts[1:]:
-        send([q0], sem, here(0), helpers, [there] * 2, "l0", inner)
-    og = D("y", [g0], "dog0", T.sld1[0], T.g0c[:])
+    to = [[h[0] for h in helpers if h[1] == k] for k in (0, 1)]
+    call([q0[0]], [("hc", inner, T.hw[:, hc[0]].bitcast(u8), to[0], [T.hr[:].bitcast(u8)] * 2)], "l0")
+    call([g0], [("r0", engs, T.g0c[:], all_, [T.sld1[rel(d, i)] for i in others])])
+    call([q0[1]], [("hc", engs, T.hw[:, hc[1]].bitcast(u8), to[1], [T.hr[:].bitcast(u8)] * 2)], "l0")
+    call([], [("hk", inner[4 * k:4 * k + 4], T.hws[:, hc[k]], to[k], [T.hrs[:]] * 2) for k in (0, 1)], "l0")
+    og = D("y", [g0], "dog0", T.sld1[N - 1], T.g0c[:])
 
-    def places(n, lo, hb, tl, hm, po):
-        a1 = V(ts, [n[0]], lo, n[1], 127, None, A.bitwise_and)
-        a2 = V(ts, [n[0]], hb, n[1], 7, 1, A.logical_shift_right, A.bitwise_and)
-
-        def rest():
-            a3 = V(tt, [a1], tl, n[1], lo, A.add)
-            a4 = V(ts, [a2], hm, hb, -127.0, None, A.mult)
-            return V(tt, [a3, a4], po, tl, hm, A.add)
-        return rest
-
-    def listed(t, dep):
-        o = slice(32 * t - 32, 32 * t)
-        x = V(ts, [dep], T.pa[:, o], T.pt[:, o], float(2048 - P * d), None, A.add)
-        x = V(ts, [x], T.np[:, o], T.pa[:, o], 2047, None, A.bitwise_and)
-        of = V(tc, [x], T.of[:, o], T.np[:, o])
-        x = places((x, T.np[:, o]), T.lo[:, o], T.hb[:, o], T.tl[:, o], T.hm[:, o], T.po[:, o])()
-        return of, V(tc, [x], T.op[:, o], T.po[:, o])
-
-    def row(t, of):
-        return S([gi, io, of], T["nr%d" % t][:], T.iot[:].indirect(T.of[:, 32 * t - 32:32 * t]), F.Copy, scale=U)
-
-    def deltas(t, nr):
-        r, v = T["nr%d" % t], T["vd%d" % t]
-        z = V(tt, [nr], v[:, 0:511], r[:, 0:511], r[:, 1:512], A.subtract)
-        return V(tc, [z], v[:, 3:512:4], r[:, 3:512:4])
-
-    nr, vd, fl0, ops = {}, {}, {}, {}
-    of1, ops[1] = listed(1, p1)
-    nr[1] = row(1, of1)
-    ic, fc = T.ic, T.fc
-    b1 = V(ts, [gp], ic[:, 1:2], ic[:, 0:1], 7, None, A.bitwise_and)
-    b4 = V(ts, [gp], ic[:, 4:5], ic[:, 0:1], 3, None, A.logical_shift_right)
-    b5 = V(ts, [gp], ic[:, 5:6], ic[:, 0:1], 15, None, A.bitwise_and)
-    b2 = V(ts, [b1], ic[:, 2:3], ic[:, 1:2], float(N - d), None, A.add)
-    b3 = V(ts, [b2], ic[:, 3:4], ic[:, 2:3], 7, None, A.bitwise_and)
-    fl0[1] = V(ms, [], T.fl1[:, 0:512:4], 0.0)
-    b6 = V(tc, [b3, b4, b5], fc[:, 0:3], ic[:, 3:6])
-    rh = V(tc, [gij], T.rh[:], T.ij[:])
-    c1 = V(ts, [b6], fc[:, 3:4], fc[:, 0:1], -256.0 * U, -127.5 * U, A.mult, A.add)
-    c2 = V(ts, [b6], fc[:, 4:5], fc[:, 0:1], 0.0, -100.0, A.is_equal, A.mult)
-    c4 = V(ts, [b6], fc[:, 10:11], fc[:, 0:1], 0.0, None, A.is_equal)
+    w = slice(0, 127)
+    x = V(ts, [p1, p2], T.pa[:, w], T.pt[:, B0:B0 + 127], float(2048 - P * (d + 1)), 2.0, A.add, A.mult)
+    a1 = V(ts, [x], T.lo[:, w], T.pa[:, w], 254, None, A.bitwise_and)
+    a2 = V(ts, [x], T.hb[:, w], T.pa[:, w], 8, 1, A.logical_shift_right, A.bitwise_and)
+    a3 = V(ts, [x], T.wq2[:, w], T.pa[:, w], 1, OWN, A.logical_shift_right, A.bitwise_and)
+    a4 = V(ts, [x], T.np[:, w], T.pa[:, w], 1, 2047, A.logical_shift_right, A.bitwise_and)
+    a5 = V(tt, [a1, a2], T.tl[:, w], T.lo[:, w], T.hb[:, w], A.add)
+    a6 = V(ts, [a3], T.wg[:, w], T.wq2[:, w], GAP / P, None, A.mult)
+    a7 = V(tt, [a5, a3], T.s2[:, w], T.tl[:, w], T.wq2[:, w], A.add)
+    a8 = V(tt, [a6, a4], T.s2[:, 128:255], T.wg[:, w], T.np[:, w], A.add)
+    for y in (0, 2, 4, 6):
+        x1 = V(tp, [a7, a8], T.t1[:, 16 * y:16 * y + 32], T.s2[:, y:256:8])
+    for k in range(4):
+        u, pi = k // 2, k % 2
+        x2 = S([x1], T.t2[:, 32 * k:32 * k + 32], T.t1[:, 64 * u + pi:64 * u + 64:2], F.Copy)
+    for k in range(4):
+        xn = V(tp, [x1], T.nt[:, 32 * k:32 * k + 32], T.t1[:, k:128:4])
     dup = V(ts, [b6, giy], T.dup[:], T.iy[:], fc[:, 2:3], None, A.add)
-    nbc = V(tt, [c1, c2], fc[:, 5:6], fc[:, 3:4], fc[:, 4:5], A.add)
-    nq = S([nr[1], c4], T.nq[:], T.nr1[:, 0:512:4], F.Copy, scale=fc[:, 10:11])
-    r2 = V(ms, [], T.rsb[:, 0:256], BIG)
-    sb0 = V(ms, [], T.sb[:], 0.0)
-    rsb = V(ms, [r2], T.rsb[:, 0:256:16], -BIG)
-    qa = V(qz, [da], T.aq[:], T.aqs[:], T.at[:])
-    vd[1] = deltas(1, nr[1])
+    for k in range(3):
+        V(tt, [xn], T.vd[:, k:64:4], T.nt[:, 32 * k + 16:32 * k + 32], T.nt[:, 32 * k + 48:32 * k + 64], A.subtract)
+    for k in range(4):
+        u, ka = k // 2, k % 2
+        xd = V(tp, [x2], T.dl[:, 32 * k:32 * k + 32], T.t2[:, 64 * u + ka:64 * u + 64:2])
+    V(tc, [xn], T.vd[:, 3:64:4], T.nt[:, 112:128])
+    for k in range(4):
+        u, ka = k // 2, k % 2
+        ops = V(tc, [xd], T.op[:, 2 * ka + u:64:4], T.dl[:, 32 * k:32 * k + 16])
+    vd = V(ts, [xn, xz], T.xw[:, 67:128:4], T.nt[:, 16:32], -7 * GAP, None, A.add)
+    l1 = V(ts, [c5, gix], T.l1[:], T.ix[:], fc[:, 9:10], None, A.add)
+    qa = []
+
+    def tile_a():
+        if len(qa) < 4:
+            i = len(qa)
+            qa.append(V(qz, [da], T.aq[:, 128 * i:128 * i + 128], T.aqs[:, 128 * i:128 * i + 128], T.at[:, 512 * i:512 * i + 512]))
+
+    def places(dep, n, lo, hb, tl, hm, po, out):
+        a1 = V(ts, [dep], lo, n, 127, None, A.bitwise_and)
+        a2 = V(ts, [dep], hb, n, 7, 1, A.logical_shift_right, A.bitwise_and)
+        a3 = V(tt, [a1], tl, n, lo, A.add)
+        a4 = V(ts, [a2], hm, hb, -127.0, None, A.mult)
+        return V(tc, [V(tt, [a3, a4], po, tl, hm, A.add)], out, po)
 
     def spread(land, deps, sems):
         for k in range(8):
@@ -260,85 +271,75 @@ def rank_program(g, core, T, topo):
         return [(n, total[n]) for n in sems]
 
     def choose(t, deps):
-        ga_, mx_, fl_, cn_ = T["ga%d" % t], T["mx%d" % t], T["fl%d" % t], T["cn%d" % t]
-        deps = deps + [ops[t]]
-        x1 = V(tc, deps, ga_[:, 0:256], T.sc[:].indirect(T.op[:, 32 * t - 32:32 * t - 16]))
-        x2 = S(deps, ga_[:, 256:512], T.sc[:].indirect(T.op[:, 32 * t - 16:32 * t]), F.Copy)
-        m = V(scan, [x1, x2, rs], mx_[:], T.rs[:], ga_[:], -BIG, A.min, A.max)
-        for k in (1, 2, 3):
-            f = V(tt, [m, fl0[t]], fl_[:, k:512:4], ga_[:, k:512:4], mx_[:, k - 1:512:4], A.is_le)
-        return V(scan, [f, vd[t]], cn_[:], fl_[:], T["vd%d" % t][:], 0.0, A.mult, A.add), x1, x2
+        ga, tg, mx, fl, xd, xr = [T[n + str(t)] for n in ("ga", "tg", "mx", "fl", "xd", "xr")]
+        o = 32 * t - 32
+        x1 = V(tc, deps + [ops], ga[:, 0:256], T.sc[:].indirect(T.op[:, o:o + 16]))
+        x2 = S(deps + [ops], ga[:, 256:512], T.sc[:].indirect(T.op[:, o + 16:o + 32]), F.Copy)
+        tile_a()
+        V(tp, [x1], tg[:, 32:288], ga[:, 0:256])
+        x = V(tp, [x2], tg[:, 288:544], ga[:, 256:512])
+        tile_a()
+        x = V(scan, [x, rs, t0[1]], mx[:], tg[:, 16:528:16], T.rs[:], -BIG, A.max, A.min)
+        tile_a()
+        x = V(tt, [x], fl[:], tg[:, 32:544:16], mx[:], A.is_le)
+        tile_a()
+        x = V(scan, [x, vd], T.xw[:, o:o + 32], fl[:], T.vd[:, o:o + 32], 0.0, A.mult, A.add)
+        y1 = V(tc, [x, l1], xd[:, 0:128], T.xw[:, o:128].indirect(T.l1[:, 0:8]))
+        y2 = S([x, l1], xd[:, 128:256], T.xw[:, o:128].indirect(T.l1[:, 8:16]), F.Copy)
+        V(tp, [y1], xr[:, 0:128], xd[:, 0:128])
+        return V(tp, [y2], xr[:, 128:256], xd[:, 128:256]), x1, x2
 
-    def whole(t, n, lists, out, deps):
-        cc, cct, cx, cn = T["cc%d" % t], T["cct%d" % t], T["cx%d" % t], T["cn%d" % t]
-        w, k = n // 2, lists.shape[1] // 2
-        x = V(tc, deps, cc[:], cn[:, 3:512:4])
-        x = V(tp, [x], cct[:], cc[:])
-        x1 = V(tc, [x], cx[:, 0:w], cct[:].indirect(lists[:, 0:k]))
-        x2 = S([x], cx[:, w:n], cct[:].indirect(lists[:, k:2 * k]), F.Copy)
-        return V(tp, [x1, x2], out, cx[:])
+    def mask(t, dep):
+        return V(ts, [dep, cm], T["mk%d" % t][:], T["xr%d" % t][:], MAGIC, fc[:, 4:5], A.add, A.is_equal)
 
-    def keep1(c, deps):
-        x = S(deps + [nbc], T.ad1[:, 0:128], c, F.Abs, bias=fc[:, 5:6])
-        mk = V(ts, [x], T.mk1[:, 0:128], T.ad1[:, 0:128], 128.0 * U, None, A.is_lt)
-        x = V(scan, [mk, zr], T.ct1[:, 0:128], T.mk1[:, 0:128], T.zer[:, 0:128], 0.0, A.add, A.add)
-        y = V(tt, [mk] + deps, T.mc[:], T.mk1[:, 0:128], c, A.mult)
-        x = V(tp, [x], T.ta[:], T.ct1[:, 96:128])
-        y = V(tt, [y, nq], T.mn[:], T.mc[:], T.nq[:], A.add)
-        y = S([y, dup], T.exm[:], T.mn[:].indirect(T.dup[:, 0:16]), F.Copy)
-        x = V(tc, [x, sb0], T.sb[:, 16:32], T.ta[:, 0:16])
-        x = V(tp, [x], T.tb[:], T.sb[:])
-        x = V(ts, [x], T.k2[:], T.ct1[:, 0:128], T.tb[:, 31:32], float(CAP), A.add, A.is_le)
-        return V(tt, [x, y], T.ex1[:, 0:256], T.k2[:].indirect(T.dup[:, 0:16]), T.exm[:], A.mult)
+    def values(t, dep):
+        return S([dep, nb, dup], T["bd%d" % t][:], T["xr%d" % t][:].indirect(T.dup[:]), F.Abs, bias=fc[:, 6:7], scale=U)
 
-    def onto(t, deps):
-        w = P * t
-        x = V(tp, deps, T["tr%d" % t][:, 0:w], T["ex%d" % t][:, 0:w])
-        return V(scan, [x, rsb], T["mr%d" % t][:, 0:w], T.rsb[:, 0:w], T["tr%d" % t][:, 0:w], -BIG, A.min, A.max)
+    def back(t, deps, op):
+        x = V(tt, deps, T["yy%d" % t][:], T["ct%d" % t][:].indirect(T.dup[:]), T["bd%d" % t][:], op)
+        x = V(tp, [x], T["yt%d" % t][:], T["yy%d" % t][:])
+        return V(scan, [x, rsb], T["mr%d" % t][:], T.rsb[:], T["yt%d" % t][:], BIG, A.max, A.min)
 
     def states(x, xs, banks, et, h, tm, q, qs, edep, picks, between=None):
         m, s, out = {}, {}, []
         for k in (0, 1):
             for i in range(4):
-                m[k, i] = MM(picks[k] + [qa], banks[k][:, 512 * i:512 * i + HALF], T.aq[:, 128 * i:128 * i + 128], T.aqs[:, 128 * i:128 * i + 128],
+                m[k, i] = MM(picks[k] + qa, banks[k][:, 512 * i:512 * i + HALF], T.aq[:, 128 * i:128 * i + 128], T.aqs[:, 128 * i:128 * i + 128],
                              x[:, HALF * k:HALF * k + HALF], xs[:, HALF * k:HALF * k + HALF])
         for k in (0, 1):
             for i in range(4):
-                o = P * i + HALF * k
-                s[k, i] = S([m[k, i]], tm[:, o:o + HALF], banks[k][:, 512 * i:512 * i + HALF], F.Copy, scale=0.05)
+                s[k, i] = S([m[k, i]], tm[:, 512 * k + i:512 * k + 512:4], banks[k][:, 512 * i:512 * i + HALF], F.Copy, scale=0.05)
             if k == 0 and between is not None:
                 between()
-        for k in (0, 1):
-            for i in range(4):
-                o = P * i + HALF * k
-                c = slice(4 * HALF * k + i, 4 * HALF * (k + 1), 4)
-                a = V(tt, [s[k, i], edep], h[:, c], tm[:, o:o + HALF], et[:, c], A.add)
-            out.append(V(qz, [a], q[:, HALF * k:HALF * k + HALF], qs[:, HALF * k:HALF * k + HALF], h[:, 4 * HALF * k:4 * HALF * (k + 1)]))
+        for i in range(4):
+            a = V(tt, [s[0, i], edep], h[:, i:512:4], tm[:, i:512:4], et[:, i:512:4], A.add)
+        out.append(V(qz, [a], q[:, 0:HALF], qs[:, 0:HALF], h[:, 0:512]))
+        a = V(tt, [s[1, 3]], h[:, 512:1024], tm[:, 512:1024], et[:, 512:1024], A.add)
+        out.append(V(qz, [a], q[:, HALF:P], qs[:, HALF:P], h[:, 512:1024]))
         return out
 
-    got = spread(T.sld1, [og, ("r0", 7 * neng), c0, sc0], ("ds0", "ds1"))
+    got = spread(T.sld1, [og, ("r0", 7 * neng), c6], ("ds0", "ds1"))
+    own = slice(OWN, OWN + P)
+    there = slice(P * rel(d, mate[0]), P * rel(d, mate[0]) + P)
+    call(got, [("hh", engs, T.hw[:, own].bitcast(u8), [cores[mate[0]]], [T.hw[:, there].bitcast(u8)])], "l0")
+    call(got, [("hh", engs, T.hws[:, own], [cores[mate[0]]], [T.hws[:, there]])], "l0")
     e1 = D("y", got, "de1", T.e1t[:], T.e1[:, :])
-    for k in range(8):
-        p2 = D("y", [], "dp2", T.pt[16 * k:16 * k + 16, 32:64], T.p2[:, 32 * (k % 2):32 * (k % 2) + 32])
-    e2 = D("y", [], "de2", T.e2t[:], T.e2[:, :])
-    dw = D("y", [], "dw", T.wt[:], T.w[:, :])
     ch, g0v, g0s = choose(1, got)
-    cr = whole(1, 128, T.rh, T.cr1[:], [ch, rh])
-    z = onto(1, [keep1(T.cr1[:], [cr])])
-    o1 = V(ts, [z], T.ofx1[:, 0:8], T.mr1[:, 7:256:32], 4096.0, None, A.mult)
-    o2 = V(ts, [z], T.ofx1[:, 8:16], T.mr1[:, 23:256:32], 4096.0, None, A.mult)
-    arr = [("h%d" % i, (PIECES + 1) * neng) for i in others]
+    bv = values(1, ch)
+    x = V(scan, [mask(1, ch), zr], T.ct1[:], T.mk1[:], T.zer[:], -float(CAP), A.add, A.add)
+    z = back(1, [x, bv], A.max)
+    o1 = V(ts, [z], T.ofx1[:], T.mr1[:, 7:256:16], 4096.0, None, A.mult)
+    arr = [("hh", (6 * 4 + 2) * neng)]
     tj = T.tj
-    ji = V(tc, [o2], tj[:, 0:16], T.ofx1[:])
-    rest = places((ji, tj[:, 0:16]), tj[:, 16:32], tj[:, 32:48], tj[:, 48:64], tj[:, 64:80], tj[:, 80:96])
 
     def pick(x, xs, w, ws, o, k, deps):
         c = slice(HALF * k, HALF * k + HALF)
         a = V(tc, deps, x[:, c].bitcast(u32), w.bitcast(u32).indirect(o[:, 8 * k:8 * k + 8]))
         return [a, S(deps, xs[:, c], ws.indirect(o[:, 8 * k:8 * k + 8]), F.Copy)]
 
-    picks = [pick(T.x1, T.x1s, T.hw[:], T.hws[:], T.ofx1, k, [o1, o2] + arr) for k in (0, 1)]
-    os1 = V(tc, [rest()], T.ofs1[:], tj[:, 80:96])
+    ji = V(ts, [z], tj[:, 0:16], T.mr1[:, 7:256:16], 4096.0, None, A.mult)
+    picks = [pick(T.x1, T.x1s, T.hw[:], T.hws[:], T.ofx1, k, [o1] + arr) for k in (0, 1)]
+    os1 = places(ji, tj[:, 0:16], tj[:, 16:32], tj[:, 32:48], tj[:, 48:64], tj[:, 64:80], tj[:, 80:96], T.ofs1[:])
     srs = []
 
     def chosen_scores():
@@ -346,94 +347,64 @@ def rank_program(g, core, T, topo):
         for k in (0, 1):
             srs.append(D("y", [srs[0]], "dsc", T.scc[:, k:k + 1], T.scr1[0:1, HALF * k:HALF * k + HALF]))
 
-    q1 = states(T.x1, T.x1s, (T.pr, T.ps), T.e1t, T.h1, T.tm1, T.hq, T.hqs, e1, picks, chosen_scores)
+    q1 = states(T.x1, T.x1s, (T.pr, T.ps), T.e1t, T.h1, T.tm1, T.hq, T.hqs, e1, [p + [g0] for p in picks], chosen_scores)
     for k in (0, 1):
         mg = scores([q1[k]], T.hq[:, HALF * k:HALF * k + HALF], T.hqs[:, HALF * k:HALF * k + HALF], T.pr[:, 512 * k:512 * k + 128])
     g1 = V(tt, [mg, srs[2]], T.g1c[:], T.pr[:, 0:1024:512], T.scc[:], A.add)
 
-    send([g1], "rg", T.g1c[:], all_, [T.sld2[rel(d, i)] for i in others])
-    og = D("y", [g1], "dog1", T.sld2[0], T.g1c[:])
-    of2, ops[2] = listed(2, p2)
-    nr[2] = row(2, of2)
-    dup4 = V(ts, [b6, giy], T.dup4[:], T.iy[:], fc[:, 2:3], 4.0, A.add, A.mult)
-    fl0[2] = V(ms, [], T.fl2[:, 0:512:4], 0.0)
-    i5c = V(ts, [b6], fc[:, 6:7], fc[:, 0:1], 512.0, None, A.mult)
-    c3 = V(ts, [b6], fc[:, 7:8], fc[:, 0:1], 512.0 + 256.0 * U, 1.0, A.mult, A.add)
-    rj = V(tc, [giz], T.rj[:], T.iz[:])
-    t0c = V(tt, [c3], fc[:, 8:9], fc[:, 7:8], fc[:, 1:2], A.add)
-    r2 = V(ms, [], T.rsb[:, 256:512], BIG)
-    t1c = V(ts, [t0c], fc[:, 9:10], fc[:, 8:9], -1.0, -16.0, A.mult, A.add)
-    cz = V(ms, [], T.cr2[:, 0:32], 0.0)
-    vd[2] = deltas(2, nr[2])
-    z = S([nr[2], dup4], T.nx2[:], T.nr2[:].indirect(T.dup4[:, 0:16]), F.Copy)
-    z = V(tp, [z], T.nt2[:], T.nx2[:])
-    rsb = V(ms, [r2], T.rsb[:, 256:512:16], -BIG)
-    n0 = V(ts, [z], T.ti[:, 0:8], T.nt2[:, 0:256:32], 4096.0, None, A.mult)
-    n0 = V(ts, [z], T.ti[:, 8:16], T.nt2[:, 16:256:32], 4096.0, None, A.mult)
-    q1b = V(qz, q1, T.w2[:, 0:P], T.w2s[:, 0:P], T.h1[:])
-    qw = V(qz, [dw], T.wq[:], T.wqs[:], T.wt[:])
-    got = spread(T.sld2, [og, ("rg", 7 * neng), g0v, g0s, srs[0]], ("ds2", "ds3"))
-
-    ch = choose(2, got)[0]
-    cr_ = T.cr2[:, 32:288]
-    cr = whole(2, 256, T.rj, cr_, [ch, rj])
-    x = S([cr, nbc], T.ad2[:], cr_, F.Abs, bias=fc[:, 5:6])
-    y = V(tt, [cr, cz], T.dc[:], cr_, T.cr2[:, 31:287], A.subtract)
-    mk = V(ts, [x], T.mk2[:], T.ad2[:], 128.0 * U, None, A.is_lt)
-    z = V(scan, [mk, y, i5c], T.ct2[:], T.mk2[:], T.dc[:], fc[:, 6:7], A.add, A.add)
-    zz = V(tt, [z], T.zz2[:], T.mk2[:], T.ct2[:], A.mult)
-    y1 = S([zz, t1c], T.d1[:], T.zz2[:], F.Identity, bias=fc[:, 9:10])
-    y0 = V(ts, [zz, t0c], T.d0[:], T.zz2[:], fc[:, 8:9], None, A.subtract)
-    y0 = V(red, [y0], T.rv[:, 0:1], T.d0[:], AxisListType.X, A.min, apply_absolute_value=True)
-    y1 = V(red, [y1], T.rv[:, 1:2], T.d1[:], AxisListType.X, A.min, apply_absolute_value=True)
-    rq = V(ts, [y0, y1], T.rq[:], T.rv[:], 255.0 * U, 4096.0, A.min, A.mult)
-    send([rq], "rr", T.rq[:], all_, [T.rqs[:, 2 * rel(d, i):2 * rel(d, i) + 2] for i in others])
-    for k in range(8):
-        D("ys"[k % 2], [("rr", 7 * neng)], ("dofq", "dofs")[k % 2], T.ofq[16 * k:16 * k + 16, 2:16], T.rqs[d:128:8, 2:16])
-    oq = [("dofq", 64), ("dofs", 64)]
-    z = V(tc, [zz, dup], T.ex2[:], T.zz2[:].indirect(T.dup[:]))
-    z = onto(2, [z])
-    ti = T.ti
-    zi = V(ts, [z], ti[:, 16:32], T.mr2[:, 7:512:32], 4096.0, None, A.mult)
-    ky = V(ts, [zi], ti[:, 48:64], ti[:, 16:32], 12, 511, A.logical_shift_right, A.bitwise_and)
-    ci = V(ts, [zi], ti[:, 32:48], ti[:, 16:32], 4095, None, A.bitwise_and)
-    kq = V(ts, [zi], ti[:, 112:128], ti[:, 16:32], 21, None, A.logical_shift_right)
-    kf = V(ts, [ky], ti[:, 64:80], ti[:, 48:64], float(CAP), None, A.is_le)
-    pc = V(tc, oq + q1, T.sp[:].bitcast(u32), T.hq[:].bitcast(u32).indirect(T.ofq[:, 2:16]))
-    pk = S(oq + q1, T.sps[:], T.hqs[:].indirect(T.ofq[:, 2:16]), F.Copy)
-    ca, cb = [], []
-    for i in others:
-        a, b = CAP * (rel(i, d) - 1), P + CAP * (rel(d, i) - 1)
-        ca.append((T.sp[:, a:a + CAP].bitcast(u8), T.w2[:, b:b + CAP].bitcast(u8)))
-        cb.append((T.sps[:, a:a + CAP], T.w2s[:, b:b + CAP]))
-    send_each([pc], "rc", ca)
-    send_each([pk], "rc", cb)
-    kc = V(tt, [kf, ci], ti[:, 80:96], ti[:, 64:80], ti[:, 32:48], A.mult)
-    x = V(ts, [kq], ti[:, 128:144], ti[:, 112:128], 32.0, None, A.mult)
-    cf = V(tt, [kc, n0], ti[:, 96:112], ti[:, 80:96], ti[:, 0:16], A.max)
-    x = V(tt, [x, ky], ti[:, 144:160], ti[:, 128:144], ti[:, 48:64], A.add)
-    x = V(tt, [x, kf], ti[:, 160:176], ti[:, 144:160], ti[:, 64:80], A.mult)
-    y = V(ts, [x], ti[:, 176:192], ti[:, 160:176], 0.0, 223.0, A.is_gt, A.mult)
-    x = V(tt, [y], ti[:, 192:208], ti[:, 160:176], ti[:, 176:192], A.add)
-    x = V(tt, [x], ti[:, 208:224], ti[:, 192:208], ti[:, 0:16], A.max)
-    ox2 = V(tc, [x], T.ofx2[:], ti[:, 208:224])
-    jp = places((cf, ti[:, 96:112]), ti[:, 224:240], ti[:, 240:256], tj[:, 96:112], tj[:, 112:128], tj[:, 128:144])()
-    os2 = V(tc, [jp], T.ofs2[:], tj[:, 128:144])
+    call([g1], [("rg", engs, T.g1c[:], all_, [T.sld2[rel(d, i)] for i in others])])
+    og = D("y", [g1], "dog1", T.sld2[N - 1], T.g1c[:])
+    q1b = V(qz, q1, T.w2[:, P:2 * P], T.w2s[:, P:2 * P], T.h1[:])
 
     def absolute(x, n, a, b, out):
-        x = V(ts, [x], a, n, float(P * d), None, A.add)
+        x = V(ts, [x], a, n, float(P * (d + 1)), None, A.add)
         x = V(ts, [x], b, a, 2047, None, A.bitwise_and)
         return V(tc, [x], out, b)
 
-    oa1 = absolute(ji, tj[:, 0:16], tj[:, 144:160], tj[:, 160:176], T.ofa1[:])
-    oa2 = absolute(cf, ti[:, 96:112], tj[:, 176:192], tj[:, 192:208], T.ofa2[:])
-    sr2 = S([os2], T.scr2[:], T.sc[:].indirect(T.ofs2[:]), F.Copy)
-    c1r = S([oa1, gi, io], T.chr1[:], T.iot[:].indirect(T.ofa1[:]), F.Copy)
-    c2r = S([oa2], T.chr2[:], T.iot[:].indirect(T.ofa2[:]), F.Copy)
-    D("s", [c1r], "dch", T.ch[0:1, :], T.chr1[0:1, :])
-    D("s", [c2r], "dch", T.ch[1:2, :], T.chr2[0:1, :])
+    oa1 = absolute(ji, tj[:, 0:16], tj[:, 144:160], tj[:, 160:176], T.cf[:, 0:16])
+    got = spread(T.sld2, [og, ("rg", 7 * neng), g0v, g0s, srs[0]], ("ds2", "ds3"))
+    e2 = D("y", got, "de2", T.e2t[:], T.e2[:, :])
+    dw = D("y", [], "dw", T.wt[:], T.w[:, :])
 
-    picks = [pick(T.x2, T.x2s, T.w2[:, 0:480], T.w2s[:, 0:480], T.ofx2, k, [("rc", 14), ox2, q1b]) for k in (0, 1)]
+    ch = choose(2, got)[0]
+    y = S([ch, c2], T.b2[:], T.xr2[:], F.Abs, bias=fc[:, 7:8], scale=U)
+    bv = values(2, ch)
+    mk = mask(2, ch)
+    x = V(scan, [mk, zr, c3], T.cq2[:], T.mk2[:], T.zer[:], fc[:, 8:9], A.add, A.add)
+    zz = V(tt, [x, y], T.zz[:], T.cq2[:], T.b2[:], A.add)
+    y1 = S([zz], T.z2[:], T.zz[:], F.Abs, bias=-16.0)
+    y0 = V(red, [zz], T.rv[:, 0:1], T.zz[:], AxisListType.X, A.min, apply_absolute_value=True)
+    y1 = V(red, [y1], T.rv[:, 1:2], T.z2[:], AxisListType.X, A.min)
+    rq = V(ts, [y0, y1], T.rq[:], T.rv[:], 255.0 * U, 4096.0, A.min, A.mult)
+    call([rq], [("rr", engs, T.rq[:], all_, [T.rqs[:, 2 * rel(d, i):2 * rel(d, i) + 2] for i in others])])
+    for k in range(8):
+        D("ys"[k % 2], [("rr", 7 * neng)], ("dofq", "dofs")[k % 2], T.ofq[16 * k:16 * k + 16, 0:14], T.rqs[d:128:8, 0:14])
+    oq = [("dofq", 64), ("dofs", 64)]
+    x = V(scan, [mk, c6], T.ct2[:], T.mk2[:], T.zer[:], fc[:, 10:11], A.add, A.add)
+    z = back(2, [x, bv], A.add)
+    ti = T.ti
+    zi = V(ts, [z], ti[:, 0:16], T.mr2[:, 7:256:16], float(CAP), 4096.0, A.add, A.mult)
+    qw = V(qz, [dw], T.wq[:], T.wqs[:], T.wt[:])
+    cf = V(ts, [zi], ti[:, 16:32], ti[:, 0:16], 2047, None, A.bitwise_and)
+    k1 = V(ts, [zi], ti[:, 32:48], ti[:, 0:16], 12, None, A.logical_shift_right)
+    k2 = V(ts, [zi], ti[:, 48:64], ti[:, 0:16], 3, CAP * (N - 1), A.logical_shift_right, A.bitwise_and)
+    pc = V(tc, oq + q1, T.sp[:].bitcast(u32), T.hq[:].bitcast(u32).indirect(T.ofq[:, 0:14]))
+    pk = S(oq + q1, T.sps[:], T.hqs[:].indirect(T.ofq[:, 0:14]), F.Copy)
+    hz = [h[0] for h in helpers if h[3]]
+    call([pk], [("hz", inner, T.sps[:], hz, [T.hs[:]] * len(hz))])
+    call([pc], [("rc", engs[k:k + 1], T.sp[:, CAP * k:CAP * k + CAP].bitcast(u8), [cores[i]],
+                 [T.w2[:, CAP * rel(d, i):CAP * rel(d, i) + CAP].bitcast(u8)]) for k, i in enumerate(others)])
+    k3 = V(ts, [cf], ti[:, 64:80], ti[:, 16:32], float(1 - OWN), 0.0, A.add, A.max)
+    k4 = V(tt, [k1, k2], ti[:, 80:96], ti[:, 32:48], ti[:, 48:64], A.add)
+    k5 = V(tt, [k3, k4], ti[:, 96:112], ti[:, 64:80], ti[:, 80:96], A.add)
+    ox2 = V(ts, [k5], T.ofx2[:], ti[:, 96:112], -1.0, None, A.add)
+    os2 = places(cf, ti[:, 16:32], tj[:, 96:112], tj[:, 112:128], tj[:, 128:144], tj[:, 208:224], tj[:, 224:240], T.ofs2[:])
+    oa2 = absolute(cf, ti[:, 16:32], tj[:, 176:192], tj[:, 192:208], T.cf[:, 16:32])
+    sr2 = S([os2], T.scr2[:], T.sc[:].indirect(T.ofs2[:]), F.Copy)
+    x = V(tp, [oa1, oa2], T.cht[:], T.cf[:])
+    D("y", [x], "dout", T.ch[:, :], T.cht[0:32, 0:16])
+
+    picks = [pick(T.x2, T.x2s, T.w2[:], T.w2s[:], T.ofx2, k, [("rc", 7 * 3), ox2, q1b]) for k in (0, 1)]
     q2 = states(T.x2, T.x2s, (T.ps, T.pr), T.e2t, T.h2, T.tm2, T.zq, T.zqs, e2, [p + [g1] for p in picks])
     for k in (0, 1):
         c = slice(HALF * k, HALF * k + HALF)
@@ -446,6 +417,6 @@ def rank_program(g, core, T, topo):
             for i in range(4):
                 D("y", [q2[k]], "dout", T.osc[4 * i:4 * i + 4, :], T.zqs[32 * i:32 * i + 4, :])
         D("y" if k == 0 else "s", [yy], ("dout", "dch")[k], T.y[:, c], T.ys[:, c])
-    D("s", [gg], "dch", T.g[0:1, :], T.go[0:1, :])
+    D("y", [gg], "dout", T.g[0:1, :], T.go[0:1, :])
 
     wait("g", [(n, total[n]) for n in total])

@@ -1,22 +1,22 @@
 from concourse.bass import DstId, RemoteDMATransfer
-from concourse.mybir import dt, AluOpType as A, AxisListType, ActivationFunctionType as F
+from concourse.mybir import dt, AluOpType as A, ActivationFunctionType as F
 
 N, P, CAP = 8, 256, 32
 HALF = P // 2
 OWN = P * (N - 1)
 BIG = 9e29
 U = 1.0 / 4096.0
-GAP = 2.0 ** 18
-MAGIC = 2.0 ** 41
+GAP = 2.0 ** 21
+MAGIC = 2.0 ** 44
 B0 = 8
 
 _f32, _i32, _u16, _bf = "float32", "int32", "uint16", "bfloat16"
 SCRATCH = {"ps": ("psum", [128, 2048], _f32), "pr": ("psum", [128, 2048], _f32), "sld1": ("dram", [8, 128, 2], _f32), "sld2": ("dram", [8, 128, 2], _f32)}
 for _d, _l in (
-        (_bf, "e0t 1024 e1t 1024 e2t 1024 ut 512 at 2048 wt 512 h1 1024 h2 1024 zer 256 mk1 256 mk2 256 ct1 256 ct2 256 cq2 256"),
-        (_f32, "tm1 1024 tm2 1024 sc 2048 rs 32 rsb 256 fc 16 s2 256 t1 128 t2 128 nt 128 dl 128 vd 64 xw 128 zz 256 z2 256 b2 256 rv 2 "
+        (_bf, "e0t 1024 e1t 1024 e2t 1024 ut 512 at 2048 wt 512 h1 1024 h2 1024 zer 256 mk1 256 mk2 256 ct1 256 ct2 256 cq 528"),
+        (_f32, "tm1 1024 tm2 1024 sc 2048 rs 32 rsb 256 fc 16 s2 256 t1 128 t2 128 nt 128 dl 128 vd 64 xw 128 zz 512 b2 256 jt 32 jo 16 "
                "scr1 256 scr2 256 scc 2 g0c 2 g1c 2 go 256 ys 256 cf 32 cht 32"),
-        (_i32, "pt 144 pa 128 np 128 lo 128 hb 128 wq2 128 tl 128 wg 128 ic 8 iy 16 ix 16 ti 256 tj 256"),
+        (_i32, "pt 144 pa 128 np 128 lo 128 hb 128 wq2 128 tl 128 wg 128 ic 8 iy 16 ix 16 iz 16 rv 4 ti 256 tj 256"),
         (_u16, "op 64 l1 16 dup 16 rq 2 rqs 16 ofq 16 ofx1 16 ofs1 16 ofx2 16 ofs2 16")):
     _w = _l.split()
     for _k in range(0, len(_w), 2):
@@ -31,11 +31,8 @@ for _t in ("1", "2"):
         SCRATCH[_n + _t] = ("sbuf", [128, _c], _f32)
 
 SEMAPHORES = ["cv", "cs", "ct", "cg", "l0", "ls", "r0", "rg", "rr", "rc", "hh", "hc", "hk", "hz"]
-SEMAPHORES += ["de0", "de0b", "du", "dp1", "dp2", "da", "de1", "dw", "de2", "dog0", "dog1", "ds0", "ds1", "ds2", "ds3", "dsc", "dofq", "dofs", "dch", "dout"]
-
-
-def bits(m):
-    return bin(m).count("1")
+SEMAPHORES += ["de0", "de0b", "du", "dp1", "dp2", "da", "de1", "dw", "de2", "dog0", "dog1", "ds0", "ds1", "dsx", "ds2", "ds3", "dsc", "dofq", "dofs",
+               "dch", "dout"]
 
 
 def plan(d, cores, topo):
@@ -44,15 +41,20 @@ def plan(d, cores, topo):
     order = [(d + k) % N for k in range(1, N)]
     mate = [i for i in order if topo.mates(here, topo.chip(cores[i]))]
     plane = [i for i in order if topo.same_plane(here, topo.chip(cores[i]))]
-    far = [i for i in order if i not in mate + plane]
-    used, out = [me], []
-    for half, ranks, asked in ((0, far, order[:4]), (0, plane, []), (1, far, order[4:]), (1, plane, [])):
-        able = [h for h in topo.cores_of(me) if h not in used and (topo.die(h) == topo.die(me)) == (half == 0)
-                and all(topo.may_write(h, cores[i]) for i in ranks + asked)]
-        able.sort(key=lambda h: sum(topo.may_write(h, cores[i]) for i in order))
-        used.append(able[0])
-        out.append((able[0], half, ranks, asked))
-    return mate, out
+    far = [i for i in order if i not in plane + mate]
+    out = []
+    for half in (0, 1):
+        able = [h for h in topo.cores_of(me) if h != me and (topo.die(h) == topo.die(me)) == (half == 0)]
+        port = [h for h in able if topo.may_write(h, cores[mate[0]])]
+        rest = [h for h in able if h not in port]
+        out.append([(port[0], far), (rest[0], plane[0:2]), (rest[1], plane[2:])])
+    return mate[0], out
+
+
+def seats(s, cores, topo):
+    order = [(s + k) % N for k in range(1, N)]
+    plane = [i for i in order if topo.same_plane(topo.chip(cores[s]), topo.chip(cores[i]))]
+    return [i for i in order if i not in plane] + plane
 
 
 def dst_of(topo, c):
@@ -74,31 +76,34 @@ def feed_engines(topo, core, near, far):
 
 
 def hand_on(g, core, T, topo):
-    u8 = dt.uint8
+    cores = T.cores
     for d in range(N):
-        for h, half, ranks, asked in plan(d, T.cores, topo)[1]:
-            if h != core:
+        for half, group in enumerate(plan(d, cores, topo)[1]):
+            if core not in [h for h, r in group]:
                 continue
-            outer, inner = feed_engines(topo, T.cores[d], core, T.cores[ranks[0]])
-            es = topo.engines(core, T.cores[ranks[0]])
-            n = 0
+            ranks = dict(group)[core]
+            j = [h for h, r in group].index(core)
+            es, inner = feed_engines(topo, core, cores[d], cores[ranks[0]])
             at = [P * rel(d, i) + HALF * half for i in ranks]
-            for sem, came, here, lands in (("hc", len(inner), T.hr[:].bitcast(u8), [T.hw[:, a:a + HALF].bitcast(u8) for a in at]),
-                                           ("hk", len(inner) // 2, T.hrs[:], [T.hws[:, a:a + HALF] for a in at])):
-                g.wait_ge(T.sem[sem], came)
-                g.remote_dma_fused([RemoteDMATransfer(dst_ids=[dst_of(topo, T.cores[i]) for i in ranks], dma_engine_mask=mask_of(es), remote_sem=T.sem.hh,
-                                                      srcs=[here], dsts=lands)], local_sem=T.sem.ls)
-                n += len(es)
-            if asked:
-                g.wait_ge(T.sem.hz, len(inner))
-                ts = []
-                for k, i in enumerate(asked):
-                    a, b = CAP * rel(i, d), CAP * rel(d, i)
-                    ts.append(RemoteDMATransfer(dst_ids=[dst_of(topo, T.cores[i])], dma_engine_mask=mask_of(es[2 * k:2 * k + 2]), remote_sem=T.sem.rc,
-                                                srcs=[T.hs[:, a:a + CAP]], dsts=[T.w2s[:, b:b + CAP]]))
+            sent = 0
+            for sem, here, lands in (("hk", T.hrs[:], [T.hws[:, a:a + HALF] for a in at]),
+                                     ("hc", T.hr[:].bitcast(dt.uint8), [T.hw[:, a:a + HALF].bitcast(dt.uint8) for a in at])):
+                g.wait_ge(T.sem[sem], len(inner))
+                ts = [RemoteDMATransfer(dst_ids=[dst_of(topo, cores[i]) for i in ranks], dma_engine_mask=mask_of(es), remote_sem=T.sem.hh, srcs=[here],
+                                        dsts=lands)]
+                if sem == "hc" and j == 0:
+                    ts.append(RemoteDMATransfer(dst_ids=[dst_of(topo, h) for h, r in group[1:]], dma_engine_mask=mask_of(inner), remote_sem=T.sem.hc,
+                                                srcs=[here], dsts=[here] * (len(group) - 1)))
                 g.remote_dma_fused(ts, local_sem=T.sem.ls)
-                n += 2 * len(asked)
-            g.wait_ge(T.sem.ls, n)
+                sent += len(es) * len(ts)
+            if half == 0 and j < 2:
+                g.wait_ge(T.sem.hz, len(inner) // 2)
+                asked = seats(d, cores, topo)[4 * j:4 * j + 4]
+                g.remote_dma_fused([RemoteDMATransfer(dst_ids=[dst_of(topo, cores[i])], dma_engine_mask=mask_of(es[2 * k:2 * k + 2]), remote_sem=T.sem.rc,
+                                                      srcs=[T.hs[:, CAP * (4 * j + k):CAP * (4 * j + k + 1)]],
+                                                      dsts=[T.w2s[:, CAP * rel(d, i):CAP * rel(d, i) + CAP]]) for k, i in enumerate(asked)], local_sem=T.sem.ls)
+                sent += 2 * len(asked)
+            g.wait_ge(T.sem.ls, sent)
 
 
 def rank_program(g, core, T, topo):
@@ -145,19 +150,20 @@ def rank_program(g, core, T, topo):
         return note(Q[q].dma_start(out, in_), name, 16)
 
     tt, ts, tc = g.vector.tensor_tensor, g.vector.tensor_scalar, g.vector.tensor_copy
-    ms, qz, scan, red, tp = g.vector.memset, g.vector.quantize_mx, g.vector.tensor_tensor_scan, g.vector.tensor_reduce, g.vector.transpose
+    ms, qz, scan, tp = g.vector.memset, g.vector.quantize_mx, g.vector.tensor_tensor_scan, g.vector.transpose
     u8, u32 = dt.uint8, dt.uint32
 
     others = [(d + k) % N for k in range(1, N)]
     all_ = [cores[i] for i in others]
-    mate, helpers = plan(d, cores, topo)
-    engs, inner = feed_engines(topo, core, helpers[0][0], all_[0])
+    mate, groups = plan(d, cores, topo)
+    to = [[h for h, r in x] for x in groups]
+    engs, inner = feed_engines(topo, core, to[0][0], all_[0])
     neng = len(engs)
 
     def call(deps, transfers, local="ls"):
         wait("g", deps)
-        g.remote_dma_fused([RemoteDMATransfer(dst_ids=[dst_of(topo, c) for c in to], dma_engine_mask=mask_of(es), remote_sem=T.sem[sem], srcs=[src], dsts=dsts)
-                            for sem, es, src, to, dsts in transfers], local_sem=T.sem[local])
+        g.remote_dma_fused([RemoteDMATransfer(dst_ids=[dst_of(topo, c) for c in to_], dma_engine_mask=mask_of(es), remote_sem=T.sem[sem], srcs=[src], dsts=dsts)
+                            for sem, es, src, to_, dsts in transfers], local_sem=T.sem[local])
         total[local] = total.get(local, 0) + sum(len(t[1]) for t in transfers)
         return (local, total[local])
 
@@ -174,36 +180,17 @@ def rank_program(g, core, T, topo):
     giy = G(g.iota, [], T.iy[:], [[32, 8], [0, 2]], 0, 0)
     gix = G(g.iota, [], T.ix[:], [[4, 8], [0, 2]], 3, 0)
     ic, fc = T.ic, T.fc
-    c0 = V(ms, [], T.sc[:, 0:512], 0.0)
+
+    def fill(out, pattern, base):
+        return G(g.iota, [], out, pattern, base, 0, allow_small_or_imprecise_dtypes=True)
+
+    gs = fill(T.sc[:, 1728:2048], [[0, 320]], 0)
+    c0 = V(ms, [], T.sc[:, 0:864], 0.0)
     uz = V(ms, [], T.ut[:, 8:512], 0.0)
     b3 = V(ts, [gp], ic[:, 2:3], ic[:, 1:2], 7, None, A.bitwise_and)
     b5 = V(ts, [gp], ic[:, 4:5], ic[:, 0:1], 31, None, A.bitwise_and)
     b4 = V(ts, [gp], ic[:, 3:4], ic[:, 0:1], 3, None, A.logical_shift_right)
-    b6 = V(tc, [b3, b4, b5], fc[:, 0:3], ic[:, 2:5])
-    for k in (1, 2, 3):
-        S([c0], T.sc[:, 512 * k:512 * k + 512], T.sc[:, 0:512], F.Copy)
-
-    def fill(deps, out, value):
-        return S(deps + [c0], out, T.sc[:, 0:out.shape[1]], F.Identity, bias=value)
-
-    def col(deps, k, j, scale, bias, func=F.Identity):
-        return S(deps, fc[:, k:k + 1], fc[:, j:j + 1], func, scale=scale, bias=bias)
-
-    r1 = fill([], T.rs[:], BIG)
-    r2 = fill([], T.rsb[:], -BIG)
-    c4 = col([b6], 3, 0, 1.0, -6.0, F.Relu)
-    c1 = col([b6], 5, 0, -GAP * U, 0.0)
-    xz = fill([], T.xw[:], 0.0)
-    rs = fill([r1], T.rs[:, 0:32:4], -BIG)
-    c5 = col([c4], 9, 3, 64.0, 0.0)
-    rsb = fill([r2], T.rsb[:, 0:256:16], BIG)
-    zr = fill([], T.zer[:], 0.0)
-    cm = col([b6], 4, 0, GAP, MAGIC)
-    nb = col([c4, c1], 6, 3, 7 * GAP * U, fc[:, 5:6])
-    t0 = [fill([], T["tg%d" % t][:, 0:32], 0.0) for t in (1, 2)]
-    c2 = col([b6], 7, 0, -(GAP + P) * U, 0.0)
-    c3 = col([b6], 8, 1, -1.0, -1.0)
-    c6 = col([c4], 10, 3, CAP + 0.5, -float(CAP))
+    sz = S([c0], T.sc[:, 864:1728], T.sc[:, 0:864], F.Copy)
 
     def scores(deps, w, ws, ps):
         return MM(deps, ps, w, ws, T.uq[:], T.uqs[:])
@@ -211,19 +198,41 @@ def rank_program(g, core, T, topo):
     hc = [slice(OWN + HALF * k, OWN + HALF * k + HALF) for k in (0, 1)]
     q0 = [V(qz, [e0[0]], T.hw[:, hc[0]], T.hws[:, hc[0]], T.e0t[:, 0:512])]
     quq = V(qz, [uu, uz], T.uq[:], T.uqs[:], T.ut[:])
+    b6 = V(tc, [b3, b4, b5], fc[:, 0:3], ic[:, 2:5])
     q0.append(V(qz, [e0[1]], T.hw[:, hc[1]], T.hws[:, hc[1]], T.e0t[:, 512:1024]))
     for k in (0, 1):
         m = scores([q0[k], quq], T.hw[:, hc[k]], T.hws[:, hc[k]], T.ps[:, 512 * k:512 * k + 128])
     g0 = V(tc, [m], T.g0c[:], T.ps[:, 0:1024:512])
-    to = [[h[0] for h in helpers if h[1] == k] for k in (0, 1)]
-    call([q0[0]], [("hc", inner, T.hw[:, hc[0]].bitcast(u8), to[0], [T.hr[:].bitcast(u8)] * 2)], "l0")
+
+    def scales_out(k, a, b, es=inner):
+        call([q0[k]], [("hk", es, T.hws[:, hc[k]], to[k][a:b], [T.hrs[:]] * (b - a))], "l0")
+
+    scales_out(0, 0, 1, engs)
     call([g0], [("r0", engs, T.g0c[:], all_, [T.sld1[rel(d, i)] for i in others])])
-    call([q0[1]], [("hc", engs, T.hw[:, hc[1]].bitcast(u8), to[1], [T.hr[:].bitcast(u8)] * 2)], "l0")
-    call([], [("hk", inner[4 * k:4 * k + 4], T.hws[:, hc[k]], to[k], [T.hrs[:]] * 2) for k in (0, 1)], "l0")
+    scales_out(1, 0, 2)
+    scales_out(0, 1, 3)
+    call([], [("hc", (inner, engs)[k], T.hw[:, hc[k]].bitcast(u8), to[k][0:1], [T.hr[:].bitcast(u8)]) for k in (0, 1)], "l0")
+    scales_out(1, 2, 3)
     og = D("y", [g0], "dog0", T.sld1[N - 1], T.g0c[:])
+    jz = fill(T.jt[:, 0:8], [[0, 8]], 0)
+    xz = fill(T.xw[:], [[0, 128]], 0)
+    t0 = [fill(T["tg%d" % t][:, 0:32], [[0, 32]], 0) for t in (1, 2)]
+    rsb = fill(T.rsb[:], [[0, 16], [-8448, 16]], 8192)
+
+    def col(deps, k, j, scale, bias, func=F.Identity):
+        return S(deps, fc[:, k:k + 1], fc[:, j:j + 1], func, scale=scale, bias=bias)
+
+    c4 = col([b6], 3, 0, 1.0, -6.0, F.Relu)
+    c1 = col([b6], 5, 0, -GAP * U, 0.0)
+    cm = col([b6], 4, 0, GAP, MAGIC)
+    c5 = col([c4], 9, 3, 64.0, 0.0)
+    nb = col([c4, c1], 6, 3, 7 * GAP * U, fc[:, 5:6])
 
     w = slice(0, 127)
     x = V(ts, [p1, p2], T.pa[:, w], T.pt[:, B0:B0 + 127], float(2048 - P * (d + 1)), 2.0, A.add, A.mult)
+    r1 = V(ms, [], T.rs[:], BIG)
+    jt = V(ts, [b6, giy], T.jt[:, 8:16], T.iy[:, 0:16:2], fc[:, 2:3], 2048.0, A.add, A.mult)
+    dup = V(ts, [b6, giy], T.dup[:], T.iy[:], fc[:, 2:3], None, A.add)
     a1 = V(ts, [x], T.lo[:, w], T.pa[:, w], 254, None, A.bitwise_and)
     a2 = V(ts, [x], T.hb[:, w], T.pa[:, w], 8, 1, A.logical_shift_right, A.bitwise_and)
     a3 = V(ts, [x], T.wq2[:, w], T.pa[:, w], 1, OWN, A.logical_shift_right, A.bitwise_and)
@@ -232,191 +241,217 @@ def rank_program(g, core, T, topo):
     a6 = V(ts, [a3], T.wg[:, w], T.wq2[:, w], GAP / P, None, A.mult)
     a7 = V(tt, [a5, a3], T.s2[:, w], T.tl[:, w], T.wq2[:, w], A.add)
     a8 = V(tt, [a6, a4], T.s2[:, 128:255], T.wg[:, w], T.np[:, w], A.add)
+    j2 = S([jt, jz], T.jt[:, 16:32], T.jt[:, 0:16], F.Identity, bias=-7 * GAP)
+    rs = V(ms, [r1], T.rs[:, 0:32:4], -BIG)
+    l1 = V(ts, [c5, gix], T.l1[:], T.ix[:], fc[:, 9:10], None, A.add)
     for y in (0, 2, 4, 6):
         x1 = V(tp, [a7, a8], T.t1[:, 16 * y:16 * y + 32], T.s2[:, y:256:8])
+    zr = V(ms, [], T.zer[:], 0.0)
     for k in range(4):
         u, pi = k // 2, k % 2
-        x2 = S([x1], T.t2[:, 32 * k:32 * k + 32], T.t1[:, 64 * u + pi:64 * u + 64:2], F.Copy)
+        x2 = V(tc, [x1], T.t2[:, 32 * k:32 * k + 32], T.t1[:, 64 * u + pi:64 * u + 64:2])
     for k in range(4):
         xn = V(tp, [x1], T.nt[:, 32 * k:32 * k + 32], T.t1[:, k:128:4])
-    dup = V(ts, [b6, giy], T.dup[:], T.iy[:], fc[:, 2:3], None, A.add)
-    for k in range(3):
-        V(tt, [xn], T.vd[:, k:64:4], T.nt[:, 32 * k + 16:32 * k + 32], T.nt[:, 32 * k + 48:32 * k + 64], A.subtract)
     for k in range(4):
         u, ka = k // 2, k % 2
         xd = V(tp, [x2], T.dl[:, 32 * k:32 * k + 32], T.t2[:, 64 * u + ka:64 * u + 64:2])
-    V(tc, [xn], T.vd[:, 3:64:4], T.nt[:, 112:128])
+    for k in range(3):
+        V(tt, [xn], T.vd[:, k:64:4], T.nt[:, 32 * k + 16:32 * k + 32], T.nt[:, 32 * k + 48:32 * k + 64], A.subtract)
+    V(tt, [xn, j2], T.vd[:, 3:64:4], T.nt[:, 112:128], T.jt[:, 0:16], A.add)
     for k in range(4):
         u, ka = k // 2, k % 2
         ops = V(tc, [xd], T.op[:, 2 * ka + u:64:4], T.dl[:, 32 * k:32 * k + 16])
-    vd = V(ts, [xn, xz], T.xw[:, 67:128:4], T.nt[:, 16:32], -7 * GAP, None, A.add)
-    l1 = V(ts, [c5, gix], T.l1[:], T.ix[:], fc[:, 9:10], None, A.add)
+    vd = V(tt, [xn, xz], T.xw[:, 67:128:4], T.nt[:, 16:32], T.jt[:, 16:32], A.add)
     qa = []
 
-    def tile_a():
-        if len(qa) < 4:
-            i = len(qa)
+    def tile_a(i):
+        if len(qa) == i:
             qa.append(V(qz, [da], T.aq[:, 128 * i:128 * i + 128], T.aqs[:, 128 * i:128 * i + 128], T.at[:, 512 * i:512 * i + 512]))
 
-    def places(dep, n, lo, hb, tl, hm, po, out):
-        a1 = V(ts, [dep], lo, n, 127, None, A.bitwise_and)
-        a2 = V(ts, [dep], hb, n, 7, 1, A.logical_shift_right, A.bitwise_and)
+    def places(dep, n, lo, tl, hm, po, out):
+        a1 = V(ts, [dep], lo, n, 255, None, A.bitwise_and)
+        yield None
         a3 = V(tt, [a1], tl, n, lo, A.add)
-        a4 = V(ts, [a2], hm, hb, -127.0, None, A.mult)
-        return V(tc, [V(tt, [a3, a4], po, tl, hm, A.add)], out, po)
+        a4 = V(ts, [a1], hm, lo, float(HALF), -255.0, A.is_ge, A.mult)
+        yield None
+        a5 = V(tt, [a3, a4], po, tl, hm, A.add)
+        yield None
+        yield V(tc, [a5], out, po)
 
     def spread(land, deps, sems):
         for k in range(8):
-            D("ys"[k % 2], deps, sems[k % 2], T.sc[16 * k:16 * k + 1, :], land[:])
+            D("ys"[k % 2], deps, sems[k % 2 if k else -1], T.sc[16 * k:16 * k + 1, :], land[:])
         return [(n, total[n]) for n in sems]
 
     def choose(t, deps):
         ga, tg, mx, fl, xd, xr = [T[n + str(t)] for n in ("ga", "tg", "mx", "fl", "xd", "xr")]
         o = 32 * t - 32
-        x1 = V(tc, deps + [ops], ga[:, 0:256], T.sc[:].indirect(T.op[:, o:o + 16]))
-        x2 = S(deps + [ops], ga[:, 256:512], T.sc[:].indirect(T.op[:, o + 16:o + 32]), F.Copy)
-        tile_a()
-        V(tp, [x1], tg[:, 32:288], ga[:, 0:256])
-        x = V(tp, [x2], tg[:, 288:544], ga[:, 256:512])
-        tile_a()
+        x1 = V(tc, deps + [ops], ga[:, 0:192], T.sc[:].indirect(T.op[:, o:o + 12]))
+        x2 = S(deps + [ops], ga[:, 192:512], T.sc[:].indirect(T.op[:, o + 12:o + 32]), F.Copy)
+        tile_a(0)
+        V(tp, [x1], tg[:, 32:224], ga[:, 0:192])
+        x = V(tp, [x2], tg[:, 224:544], ga[:, 192:512])
+        tile_a(1)
         x = V(scan, [x, rs, t0[1]], mx[:], tg[:, 16:528:16], T.rs[:], -BIG, A.max, A.min)
-        tile_a()
+        tile_a(2)
         x = V(tt, [x], fl[:], tg[:, 32:544:16], mx[:], A.is_le)
-        tile_a()
+        tile_a(3)
         x = V(scan, [x, vd], T.xw[:, o:o + 32], fl[:], T.vd[:, o:o + 32], 0.0, A.mult, A.add)
-        y1 = V(tc, [x, l1], xd[:, 0:128], T.xw[:, o:128].indirect(T.l1[:, 0:8]))
-        y2 = S([x, l1], xd[:, 128:256], T.xw[:, o:128].indirect(T.l1[:, 8:16]), F.Copy)
-        V(tp, [y1], xr[:, 0:128], xd[:, 0:128])
-        return V(tp, [y2], xr[:, 128:256], xd[:, 128:256]), x1, x2
-
-    def mask(t, dep):
-        return V(ts, [dep, cm], T["mk%d" % t][:], T["xr%d" % t][:], MAGIC, fc[:, 4:5], A.add, A.is_equal)
+        y1 = V(tc, [x, l1], xd[:, 0:96], T.xw[:, o:128].indirect(T.l1[:, 0:6]))
+        y2 = S([x, l1], xd[:, 96:256], T.xw[:, o:128].indirect(T.l1[:, 6:16]), F.Copy)
+        z1 = V(tp, [y1], xr[:, 0:96], xd[:, 0:96])
+        z2 = V(tp, [y2], xr[:, 96:256], xd[:, 96:256])
+        for z, c in ((z1, slice(0, 96)), (z2, slice(96, 256))):
+            mk = V(ts, [z, cm], T["mk%d" % t][:, c], xr[:, c], MAGIC, fc[:, 4:5], A.add, A.is_equal)
+        return z2, mk, x1, x2
 
     def values(t, dep):
         return S([dep, nb, dup], T["bd%d" % t][:], T["xr%d" % t][:].indirect(T.dup[:]), F.Abs, bias=fc[:, 6:7], scale=U)
 
     def back(t, deps, op):
-        x = V(tt, deps, T["yy%d" % t][:], T["ct%d" % t][:].indirect(T.dup[:]), T["bd%d" % t][:], op)
-        x = V(tp, [x], T["yt%d" % t][:], T["yy%d" % t][:])
-        return V(scan, [x, rsb], T["mr%d" % t][:], T.rsb[:], T["yt%d" % t][:], BIG, A.max, A.min)
+        yy, yt, mr = [T[n + str(t)] for n in ("yy", "yt", "mr")]
+        c = [slice(HALF * k, HALF * k + HALF) for k in (0, 1)]
+        x = [V(tt, deps, yy[:, c[k]], T["ct%d" % t][:].indirect(T.dup[:, 8 * k:8 * k + 8]), T["bd%d" % t][:, c[k]], op) for k in (0, 1)]
+        x = [V(tp, [x[k]], yt[:, c[k]], yy[:, c[k]]) for k in (0, 1)]
+        return [V(scan, [x[k], rsb], mr[:, c[k]], T.rsb[:, c[k]], yt[:, c[k]], BIG, A.max, A.min) for k in (0, 1)]
 
-    def states(x, xs, banks, et, h, tm, q, qs, edep, picks, between=None):
-        m, s, out = {}, {}, []
+    def states(o, od, w, ws, x, xs, banks, h, tm, et, edep, q, qs, steps, nv):
+        c = [slice(HALF * k, HALF * k + HALF) for k in (0, 1)]
+        pc, pk = [], []
+        for k in (0, 1):
+            pc.append(V(tc, od[k], x[:, c[k]].bitcast(u32), w.bitcast(u32).indirect(o[:, 8 * k:8 * k + 8])))
+            pk.append(S(od[k], xs[:, c[k]], ws.indirect(o[:, 8 * k:8 * k + 8]), F.Copy))
+            next(steps)
+        m, s, a, out = {}, {}, {}, []
         for k in (0, 1):
             for i in range(4):
-                m[k, i] = MM(picks[k] + qa, banks[k][:, 512 * i:512 * i + HALF], T.aq[:, 128 * i:128 * i + 128], T.aqs[:, 128 * i:128 * i + 128],
-                             x[:, HALF * k:HALF * k + HALF], xs[:, HALF * k:HALF * k + HALF])
-        for k in (0, 1):
-            for i in range(4):
-                s[k, i] = S([m[k, i]], tm[:, 512 * k + i:512 * k + 512:4], banks[k][:, 512 * i:512 * i + HALF], F.Copy, scale=0.05)
-            if k == 0 and between is not None:
-                between()
-        for i in range(4):
-            a = V(tt, [s[0, i], edep], h[:, i:512:4], tm[:, i:512:4], et[:, i:512:4], A.add)
-        out.append(V(qz, [a], q[:, 0:HALF], qs[:, 0:HALF], h[:, 0:512]))
-        a = V(tt, [s[1, 3]], h[:, 512:1024], tm[:, 512:1024], et[:, 512:1024], A.add)
-        out.append(V(qz, [a], q[:, HALF:P], qs[:, HALF:P], h[:, 512:1024]))
+                m[k, i] = MM([pc[k], pk[k]] + qa, banks[k][:, 512 * i:512 * i + HALF], T.aq[:, 128 * i:128 * i + 128], T.aqs[:, 128 * i:128 * i + 128],
+                             x[:, c[k]], xs[:, c[k]])
+
+        def scale(k, i):
+            to_, r = tm[:, 512 * k + 128 * i:512 * k + 128 * i + 128], banks[k][:, 512 * i:512 * i + HALF]
+            s[k, i] = V(ts, [m[k, i]], to_, r, 0.05, None, A.mult) if 4 * k + i < nv else S([m[k, i]], to_, r, F.Copy, scale=0.05)
+
+        for n in range(6):
+            scale(n // 4, n % 4)
+            if n == 0:
+                next(steps)
+        for n in range(8):
+            k, i = n // 4, n % 4
+            e = slice(512 * k + i, 512 * k + 512, 4)
+            a[n] = V(tt, [s[k, i], edep], h[:, e], tm[:, 128 * n:128 * n + 128], et[:, e], A.add)
+            if n < 2:
+                next(steps)
+            if n == 1:
+                scale(1, 2)
+                scale(1, 3)
+            if n in (4, 7):
+                k = n // 7
+                out.append(V(qz, [a[4 * k + 3]], q[:, c[k]], qs[:, c[k]], h[:, 512 * k:512 * k + 512]))
         return out
 
-    got = spread(T.sld1, [og, ("r0", 7 * neng), c6], ("ds0", "ds1"))
-    own = slice(OWN, OWN + P)
-    there = slice(P * rel(d, mate[0]), P * rel(d, mate[0]) + P)
-    call(got, [("hh", engs, T.hw[:, own].bitcast(u8), [cores[mate[0]]], [T.hw[:, there].bitcast(u8)])], "l0")
-    call(got, [("hh", engs, T.hws[:, own], [cores[mate[0]]], [T.hws[:, there]])], "l0")
-    e1 = D("y", got, "de1", T.e1t[:], T.e1[:, :])
-    ch, g0v, g0s = choose(1, got)
+    got = spread(T.sld1, [og, ("r0", 7 * neng), sz, gs], ("ds0", "ds1", "dsx"))
+    there = slice(P * rel(d, mate), P * rel(d, mate) + P)
+    call(got[2:], [("hh", engs, T.hw[:, OWN:OWN + P].bitcast(u8), [cores[mate]], [T.hw[:, there].bitcast(u8)])], "l0")
+    call([], [("hh", engs, T.hws[:, OWN:OWN + P], [cores[mate]], [T.hws[:, there]])], "l0")
+    giz = G(g.iota, [], T.iz[:], [[16, 16]], 0, 0)
+    ch, mk, g0v, g0s = choose(1, got)
+    e1 = D("y", [g0v], "de1", T.e1t[:], T.e1[:, :])
     bv = values(1, ch)
-    x = V(scan, [mask(1, ch), zr], T.ct1[:], T.mk1[:], T.zer[:], -float(CAP), A.add, A.add)
+    x = V(scan, [mk, zr], T.ct1[:], T.mk1[:], T.zer[:], -float(CAP), A.add, A.add)
     z = back(1, [x, bv], A.max)
-    o1 = V(ts, [z], T.ofx1[:], T.mr1[:, 7:256:16], 4096.0, None, A.mult)
-    arr = [("hh", (6 * 4 + 2) * neng)]
+    o1 = [V(ts, [z[k]], T.ofx1[:, 8 * k:8 * k + 8], T.mr1[:, 7 + HALF * k:HALF + HALF * k:16], 4096.0, None, A.mult) for k in (0, 1)]
+    arr = [("hh", (6 * 4 + 2) * neng), g0]
     tj = T.tj
-
-    def pick(x, xs, w, ws, o, k, deps):
-        c = slice(HALF * k, HALF * k + HALF)
-        a = V(tc, deps, x[:, c].bitcast(u32), w.bitcast(u32).indirect(o[:, 8 * k:8 * k + 8]))
-        return [a, S(deps, xs[:, c], ws.indirect(o[:, 8 * k:8 * k + 8]), F.Copy)]
-
-    ji = V(ts, [z], tj[:, 0:16], T.mr1[:, 7:256:16], 4096.0, None, A.mult)
-    picks = [pick(T.x1, T.x1s, T.hw[:], T.hws[:], T.ofx1, k, [o1] + arr) for k in (0, 1)]
-    os1 = places(ji, tj[:, 0:16], tj[:, 16:32], tj[:, 32:48], tj[:, 48:64], tj[:, 64:80], tj[:, 80:96], T.ofs1[:])
-    srs = []
+    sr1 = []
 
     def chosen_scores():
-        srs.append(S([os1], T.scr1[:], T.sc[:].indirect(T.ofs1[:]), F.Copy))
+        sr1.append(V(ts, z, tj[:, 0:16], T.mr1[:, 7:256:16], 4096.0, None, A.mult))
+        yield None
+        for k, os1 in enumerate(places(sr1[0], tj[:, 0:16], tj[:, 16:32], tj[:, 48:64], tj[:, 64:80], tj[:, 80:96], T.ofs1[:])):
+            if k < 3:
+                yield None
+        sr1.append(S([os1], T.scr1[:], T.sc[:].indirect(T.ofs1[:]), F.Copy))
         for k in (0, 1):
-            srs.append(D("y", [srs[0]], "dsc", T.scc[:, k:k + 1], T.scr1[0:1, HALF * k:HALF * k + HALF]))
+            scc = D("y", sr1[1:2], "dsc", T.scc[:, k:k + 1], T.scr1[0:1, HALF * k:HALF * k + HALF])
+        sr1.append(scc)
+        yield None
 
-    q1 = states(T.x1, T.x1s, (T.pr, T.ps), T.e1t, T.h1, T.tm1, T.hq, T.hqs, e1, [p + [g0] for p in picks], chosen_scores)
+    q1 = states(T.ofx1, [[o] + arr for o in o1], T.hw[:], T.hws[:], T.x1, T.x1s, (T.pr, T.ps), T.h1, T.tm1, T.e1t, e1, T.hq, T.hqs, chosen_scores(), 1)
     for k in (0, 1):
         mg = scores([q1[k]], T.hq[:, HALF * k:HALF * k + HALF], T.hqs[:, HALF * k:HALF * k + HALF], T.pr[:, 512 * k:512 * k + 128])
-    g1 = V(tt, [mg, srs[2]], T.g1c[:], T.pr[:, 0:1024:512], T.scc[:], A.add)
+    g1 = V(tt, [mg, sr1[2]], T.g1c[:], T.pr[:, 0:1024:512], T.scc[:], A.add)
 
     call([g1], [("rg", engs, T.g1c[:], all_, [T.sld2[rel(d, i)] for i in others])])
     og = D("y", [g1], "dog1", T.sld2[N - 1], T.g1c[:])
+    c2 = col([], 7, 0, -2.0, 0.0)
+    c6 = col([], 10, 3, CAP + 0.5, -float(CAP))
+    for k in (0, 1):
+        c7 = S([], T.cq[:, 264 * k:264 * k + 1], fc[:, 1:2], F.Identity, bias=0.5 + 16 * k)
     q1b = V(qz, q1, T.w2[:, P:2 * P], T.w2s[:, P:2 * P], T.h1[:])
+    x = V(ts, [gp], ic[:, 5:6], ic[:, 0:1], 15, None, A.bitwise_and)
+    x = V(tc, [x], fc[:, 12:13], ic[:, 5:6])
+    jo = V(ts, [x, giz], T.jo[:], T.iz[:], fc[:, 12:13], -0.5, A.add, A.mult)
 
     def absolute(x, n, a, b, out):
         x = V(ts, [x], a, n, float(P * (d + 1)), None, A.add)
         x = V(ts, [x], b, a, 2047, None, A.bitwise_and)
         return V(tc, [x], out, b)
 
-    oa1 = absolute(ji, tj[:, 0:16], tj[:, 144:160], tj[:, 160:176], T.cf[:, 0:16])
-    got = spread(T.sld2, [og, ("rg", 7 * neng), g0v, g0s, srs[0]], ("ds2", "ds3"))
+    oa1 = absolute(sr1[0], tj[:, 0:16], tj[:, 144:160], tj[:, 160:176], T.cf[:, 0:16])
+    got = spread(T.sld2, [og, ("rg", 7 * neng), g0v, g0s, sr1[1]], ("ds3", "ds2", "ds3"))
     e2 = D("y", got, "de2", T.e2t[:], T.e2[:, :])
     dw = D("y", [], "dw", T.wt[:], T.w[:, :])
 
-    ch = choose(2, got)[0]
-    y = S([ch, c2], T.b2[:], T.xr2[:], F.Abs, bias=fc[:, 7:8], scale=U)
+    ch, mk = choose(2, got)[0:2]
+    y = S([ch, c2], T.b2[:], T.xr2[:], F.Abs, bias=fc[:, 7:8], scale=2.0 / GAP)
     bv = values(2, ch)
-    mk = mask(2, ch)
-    x = V(scan, [mk, zr, c3], T.cq2[:], T.mk2[:], T.zer[:], fc[:, 8:9], A.add, A.add)
-    zz = V(tt, [x, y], T.zz[:], T.cq2[:], T.b2[:], A.add)
-    y1 = S([zz], T.z2[:], T.zz[:], F.Abs, bias=-16.0)
-    y0 = V(red, [zz], T.rv[:, 0:1], T.zz[:], AxisListType.X, A.min, apply_absolute_value=True)
-    y1 = V(red, [y1], T.rv[:, 1:2], T.z2[:], AxisListType.X, A.min)
-    rq = V(ts, [y0, y1], T.rq[:], T.rv[:], 255.0 * U, 4096.0, A.min, A.mult)
-    call([rq], [("rr", engs, T.rq[:], all_, [T.rqs[:, 2 * rel(d, i):2 * rel(d, i) + 2] for i in others])])
+    x = [V(scan, [mk, zr, c7], T.cq[:, 264 * k + 1:264 * k + 257], T.zer[:], T.mk2[:], T.cq[:, 264 * k:264 * k + 1], A.add, A.subtract) for k in (0, 1)]
+    sel = [V(scan, [x[k], y], T.zz[:, P * k:P * k + P], T.cq[:, 264 * k:264 * k + 256], T.b2[:], 0.0, A.max, A.min) for k in (0, 1)]
+    x = V(ts, sel, T.rv[:, 0:2], T.zz[:, 255:512:256], GAP / 2.0, None, A.mult)
+    cnt = V(scan, [mk, c6], T.ct2[:], T.mk2[:], T.zer[:], fc[:, 10:11], A.add, A.add)
+    x = V(ts, [x], T.rv[:, 2:4], T.rv[:, 0:2], 255, None, A.bitwise_and)
+    rq = V(tc, [x], T.rq[:], T.rv[:, 2:4])
+    call([rq], [("rr", engs, T.rq[:], all_, [T.rqs[:, 2 * j:2 * j + 2] for j in [seats(i, cores, topo).index(d) for i in others]])])
     for k in range(8):
         D("ys"[k % 2], [("rr", 7 * neng)], ("dofq", "dofs")[k % 2], T.ofq[16 * k:16 * k + 16, 0:14], T.rqs[d:128:8, 0:14])
     oq = [("dofq", 64), ("dofs", 64)]
-    x = V(scan, [mk, c6], T.ct2[:], T.mk2[:], T.zer[:], fc[:, 10:11], A.add, A.add)
-    z = back(2, [x, bv], A.add)
+    z = back(2, [cnt, bv], A.add)
     ti = T.ti
-    zi = V(ts, [z], ti[:, 0:16], T.mr2[:, 7:256:16], float(CAP), 4096.0, A.add, A.mult)
+    x = V(tt, z + [jo], T.b2[:, 0:16], T.mr2[:, 7:256:16], T.jo[:], A.add)
     qw = V(qz, [dw], T.wq[:], T.wqs[:], T.wt[:])
+    zi = V(ts, [x], ti[:, 0:16], T.b2[:, 0:16], float(CAP), 4096.0, A.add, A.mult)
     cf = V(ts, [zi], ti[:, 16:32], ti[:, 0:16], 2047, None, A.bitwise_and)
     k1 = V(ts, [zi], ti[:, 32:48], ti[:, 0:16], 12, None, A.logical_shift_right)
     k2 = V(ts, [zi], ti[:, 48:64], ti[:, 0:16], 3, CAP * (N - 1), A.logical_shift_right, A.bitwise_and)
     pc = V(tc, oq + q1, T.sp[:].bitcast(u32), T.hq[:].bitcast(u32).indirect(T.ofq[:, 0:14]))
     pk = S(oq + q1, T.sps[:], T.hqs[:].indirect(T.ofq[:, 0:14]), F.Copy)
-    hz = [h[0] for h in helpers if h[3]]
-    call([pk], [("hz", inner, T.sps[:], hz, [T.hs[:]] * len(hz))])
+    call([pk], [("hz", inner[4 * k:4 * k + 4], T.sps[:, 96 * k:96 * k + 128], [to[0][k]], [T.hs[:, 96 * k:96 * k + 128]]) for k in (0, 1)])
     call([pc], [("rc", engs[k:k + 1], T.sp[:, CAP * k:CAP * k + CAP].bitcast(u8), [cores[i]],
-                 [T.w2[:, CAP * rel(d, i):CAP * rel(d, i) + CAP].bitcast(u8)]) for k, i in enumerate(others)])
+                 [T.w2[:, CAP * rel(d, i):CAP * rel(d, i) + CAP].bitcast(u8)]) for k, i in enumerate(seats(d, cores, topo))])
     k3 = V(ts, [cf], ti[:, 64:80], ti[:, 16:32], float(1 - OWN), 0.0, A.add, A.max)
     k4 = V(tt, [k1, k2], ti[:, 80:96], ti[:, 32:48], ti[:, 48:64], A.add)
     k5 = V(tt, [k3, k4], ti[:, 96:112], ti[:, 64:80], ti[:, 80:96], A.add)
     ox2 = V(ts, [k5], T.ofx2[:], ti[:, 96:112], -1.0, None, A.add)
-    os2 = places(cf, ti[:, 16:32], tj[:, 96:112], tj[:, 112:128], tj[:, 128:144], tj[:, 208:224], tj[:, 224:240], T.ofs2[:])
+    os2 = list(places(cf, ti[:, 16:32], tj[:, 96:112], tj[:, 128:144], tj[:, 208:224], tj[:, 224:240], T.ofs2[:]))[-1]
     oa2 = absolute(cf, ti[:, 16:32], tj[:, 176:192], tj[:, 192:208], T.cf[:, 16:32])
     sr2 = S([os2], T.scr2[:], T.sc[:].indirect(T.ofs2[:]), F.Copy)
     x = V(tp, [oa1, oa2], T.cht[:], T.cf[:])
     D("y", [x], "dout", T.ch[:, :], T.cht[0:32, 0:16])
 
-    picks = [pick(T.x2, T.x2s, T.w2[:], T.w2s[:], T.ofx2, k, [("rc", 7 * 3), ox2, q1b]) for k in (0, 1)]
-    q2 = states(T.x2, T.x2s, (T.ps, T.pr), T.e2t, T.h2, T.tm2, T.zq, T.zqs, e2, [p + [g1] for p in picks])
+    q2 = states(T.ofx2, [[("rc", 7 * 3), ox2, q1b, g1]] * 2, T.w2[:], T.w2s[:], T.x2, T.x2s, (T.ps, T.pr), T.h2, T.tm2, T.e2t, e2, T.zq, T.zqs,
+                iter(range(9)), 2)
     for k in (0, 1):
         c = slice(HALF * k, HALF * k + HALF)
         m1 = MM([q2[k], qw], T.ps[:, 512 * k:512 * k + HALF], T.wq[:], T.wqs[:], T.zq[:, c], T.zqs[:, c])
         m2 = MM([q2[k]], T.ps[:, 1024 + 512 * k:1024 + 512 * k + HALF], T.uq[:], T.uqs[:], T.zq[:, c], T.zqs[:, c])
         D("y", [q2[k]], "dout", T.oc[:, 4 * HALF * k:4 * HALF * (k + 1)], T.zq[:, c].bitcast(u8))
-        yy = S([m1], T.ys[:, c], T.ps[:, 512 * k:512 * k + HALF], F.Copy)
+        yy = V(tc, [m1], T.ys[:, c], T.ps[:, 512:512 + HALF]) if k else S([m1], T.ys[:, c], T.ps[:, 0:HALF], F.Copy)
         gg = V(tt, [m2, sr2], T.go[0:1, c], T.ps[0:1, 1024 + 512 * k:1024 + 512 * k + HALF], T.scr2[0:1, c], A.add)
         if k:
             for i in range(4):
                 D("y", [q2[k]], "dout", T.osc[4 * i:4 * i + 4, :], T.zqs[32 * i:32 * i + 4, :])
-        D("y" if k == 0 else "s", [yy], ("dout", "dch")[k], T.y[:, c], T.ys[:, c])
+        D("s", [yy], "dch", T.y[:, c], T.ys[:, c])
     D("y", [gg], "dout", T.g[0:1, :], T.go[0:1, :])
 
     wait("g", [(n, total[n]) for n in total])

from concourse.bass import DstId, RemoteDMATransfer
from concourse.mybir import dt, AluOpType as A, ActivationFunctionType as F

N, P, CAP = 8, 256, 32
HALF = P // 2
OWN = P * (N - 1)
BIG = 9e29
U = 1.0 / 4096.0
GAP = 2.0 ** 21
MAGIC = 2.0 ** 44
B0 = 8

_f32, _i32, _u16, _bf = "float32", "int32", "uint16", "bfloat16"
SCRATCH = {"ps": ("psum", [128, 2048], _f32), "pr": ("psum", [128, 2048], _f32), "sld1": ("dram", [8, 128, 2], _f32), "sld2": ("dram", [8, 128, 2], _f32)}
for _d, _l in (
        (_bf, "e0t 1024 e1t 1024 e2t 1024 ut 512 at 2048 wt 512 h1 1024 h2 1024 zer 256 mk1 256 mk2 256 ct1 256 ct2 256 cq 528"),
        (_f32, "tm1 1024 tm2 1024 sc 2048 rs 32 rsb 256 fc 16 s2 256 t1 128 t2 128 nt 128 dl 128 vd 64 xw 128 zz 512 b2 256 jt 32 jo 16 "
               "scr1 256 scr2 256 scc 2 g0c 2 g1c 2 go 256 ys 256 cf 32 cht 32"),
        (_i32, "pt 144 pa 128 np 128 lo 128 hb 128 wq2 128 tl 128 wg 128 ic 8 iy 16 ix 16 iz 16 rv 4 ti 256 tj 256"),
        (_u16, "op 64 l1 16 dup 16 rq 2 rqs 16 ofq 16 ofx1 16 ofs1 16 ofx2 16 ofs2 16")):
    _w = _l.split()
    for _k in range(0, len(_w), 2):
        SCRATCH[_w[_k]] = ("sbuf", [128, int(_w[_k + 1])], _d)
for _n, _c in (("uq", 128), ("aq", 512), ("wq", 128), ("hw", 2048), ("hr", 128), ("x1", 256), ("hq", 256), ("sp", 224), ("w2", 512), ("x2", 256),
               ("zq", 256)):
    SCRATCH[_n] = ("sbuf", [128, _c], "float8_e4m3fn_x4")
    SCRATCH[_n + "s"] = ("sbuf", [128, _c], "uint8")
SCRATCH["hs"] = ("sbuf", [128, 224], "uint8")
for _t in ("1", "2"):
    for _n, _c in (("ga", 512), ("tg", 544), ("mx", 32), ("fl", 32), ("xd", 256), ("xr", 256), ("bd", 256), ("yy", 256), ("yt", 256), ("mr", 256)):
        SCRATCH[_n + _t] = ("sbuf", [128, _c], _f32)

SEMAPHORES = ["cv", "cs", "ct", "cg", "l0", "ls", "r0", "rg", "rr", "rc", "hh", "hc", "hk", "hz"]
SEMAPHORES += ["de0", "de0b", "du", "dp1", "dp2", "da", "de1", "dw", "de2", "dog0", "dog1", "ds0", "ds1", "dsx", "ds2", "ds3", "dsc", "dofq", "dofs",
               "dch", "dout"]


def plan(d, cores, topo):
    me = cores[d]
    here = topo.chip(me)
    order = [(d + k) % N for k in range(1, N)]
    mate = [i for i in order if topo.mates(here, topo.chip(cores[i]))]
    plane = [i for i in order if topo.same_plane(here, topo.chip(cores[i]))]
    far = [i for i in order if i not in plane + mate]
    out = []
    for half in (0, 1):
        able = [h for h in topo.cores_of(me) if h != me and (topo.die(h) == topo.die(me)) == (half == 0)]
        port = [h for h in able if topo.may_write(h, cores[mate[0]])]
        rest = [h for h in able if h not in port]
        out.append([(port[0], far), (rest[0], plane[0:2]), (rest[1], plane[2:])])
    return mate[0], out


def seats(s, cores, topo):
    order = [(s + k) % N for k in range(1, N)]
    plane = [i for i in order if topo.same_plane(topo.chip(cores[s]), topo.chip(cores[i]))]
    return [i for i in order if i not in plane] + plane


def dst_of(topo, c):
    rid, pid, _ = topo.addr(c)
    return DstId(rid=rid, pnc=pid)


def rel(s, r):
    return (s - r - 1) % N


def mask_of(es):
    return sum(1 << e for e in es)


def feed_engines(topo, core, near, far):
    out = topo.engines(core, far)
    return out, [e for e in topo.engines(core, near) if e not in out]


def hand_on(g, core, T, topo):
    cores = T.cores
    for d in range(N):
        for half, group in enumerate(plan(d, cores, topo)[1]):
            if core not in [h for h, r in group]:
                continue
            ranks = dict(group)[core]
            j = [h for h, r in group].index(core)
            es, inner = feed_engines(topo, core, cores[d], cores[ranks[0]])
            at = [P * rel(d, i) + HALF * half for i in ranks]
            sent = 0
            for sem, here, lands in (("hk", T.hrs[:], [T.hws[:, a:a + HALF] for a in at]),
                                     ("hc", T.hr[:].bitcast(dt.uint8), [T.hw[:, a:a + HALF].bitcast(dt.uint8) for a in at])):
                g.wait_ge(T.sem[sem], len(inner))
                ts = [RemoteDMATransfer(dst_ids=[dst_of(topo, cores[i]) for i in ranks], dma_engine_mask=mask_of(es), remote_sem=T.sem.hh, srcs=[here],
                                        dsts=lands)]
                if sem == "hc" and j == 0:
                    ts.append(RemoteDMATransfer(dst_ids=[dst_of(topo, h) for h, r in group[1:]], dma_engine_mask=mask_of(inner), remote_sem=T.sem.hc,
                                                srcs=[here], dsts=[here] * (len(group) - 1)))
                g.remote_dma_fused(ts, local_sem=T.sem.ls)
                sent += len(es) * len(ts)
            if half == 0 and j < 2:
                g.wait_ge(T.sem.hz, len(inner) // 2)
                asked = seats(d, cores, topo)[4 * j:4 * j + 4]
                g.remote_dma_fused([RemoteDMATransfer(dst_ids=[dst_of(topo, cores[i])], dma_engine_mask=mask_of(es[2 * k:2 * k + 2]), remote_sem=T.sem.rc,
                                                      srcs=[T.hs[:, CAP * (4 * j + k):CAP * (4 * j + k + 1)]],
                                                      dsts=[T.w2s[:, CAP * rel(d, i):CAP * rel(d, i) + CAP]]) for k, i in enumerate(asked)], local_sem=T.sem.ls)
                sent += 2 * len(asked)
            g.wait_ge(T.sem.ls, sent)


def rank_program(g, core, T, topo):
    d = T.rank_of(core)
    if d is None:
        hand_on(g, core, T, topo)
        return
    cores = T.cores
    Q = {"v": g.vector, "s": g.scalar, "t": g.tensor, "g": g, "y": g.sync}
    total, seen = {}, {}

    def wait(q, deps):
        need = {}
        for name, val in deps:
            need[name] = max(val, need.get(name, 0))
        for name in need:
            if seen.get((q, name), 0) < need[name]:
                Q[q].wait_ge(T.sem[name], need[name])
                seen[(q, name)] = need[name]

    def note(ins, name, n):
        ins.then_inc(T.sem[name], n)
        total[name] = total.get(name, 0) + n
        return (name, total[name])

    def V(call, deps, *args, **kw):
        wait("v", deps)
        return note(call(*args, **kw), "cv", 1)

    def S(deps, *args, **kw):
        wait("s", deps)
        return note(g.scalar.activation(*args, **kw), "cs", 1)

    def MM(deps, out, w, ws, x, xs):
        wait("t", deps)
        return note(g.tensor.matmul_mx(out, w, ws, x, xs, True, True), "ct", 1)

    def G(call, deps, *args, **kw):
        wait("g", deps)
        return note(call(*args, **kw), "cg", 1)

    def D(q, deps, name, out, in_):
        wait(q, deps)
        return note(Q[q].dma_start(out, in_), name, 16)

    tt, ts, tc = g.vector.tensor_tensor, g.vector.tensor_scalar, g.vector.tensor_copy
    ms, qz, scan, tp = g.vector.memset, g.vector.quantize_mx, g.vector.tensor_tensor_scan, g.vector.transpose
    u8, u32 = dt.uint8, dt.uint32

    others = [(d + k) % N for k in range(1, N)]
    all_ = [cores[i] for i in others]
    mate, groups = plan(d, cores, topo)
    to = [[h for h, r in x] for x in groups]
    engs, inner = feed_engines(topo, core, to[0][0], all_[0])
    neng = len(engs)

    def call(deps, transfers, local="ls"):
        wait("g", deps)
        g.remote_dma_fused([RemoteDMATransfer(dst_ids=[dst_of(topo, c) for c in to_], dma_engine_mask=mask_of(es), remote_sem=T.sem[sem], srcs=[src], dsts=dsts)
                            for sem, es, src, to_, dsts in transfers], local_sem=T.sem[local])
        total[local] = total.get(local, 0) + sum(len(t[1]) for t in transfers)
        return (local, total[local])

    e0 = [D("y", [], "de0", T.e0t[:, 0:512], T.e0[:, 0:512])]
    uu = D("s", [], "du", T.ut[:, 0:8], T.u[:, 0:8])
    e0.append(D("y", [], "de0b", T.e0t[:, 512:1024], T.e0[:, 512:1024]))
    for k in range(8):
        b = B0 - k % 2
        p1 = D("y", [], "dp1", T.pt[16 * k:16 * k + 16, b:b + 64], T.p1[:, :])
        p2 = D("s", [], "dp2", T.pt[16 * k:16 * k + 16, b + 64:b + 128], T.p2[:, :])
    da = D("y", [], "da", T.at[:], T.a[:, :])

    gp = G(g.iota, [], T.ic[:, 0:2], [[N - 1 - d, 2]], 0, 1)
    giy = G(g.iota, [], T.iy[:], [[32, 8], [0, 2]], 0, 0)
    gix = G(g.iota, [], T.ix[:], [[4, 8], [0, 2]], 3, 0)
    ic, fc = T.ic, T.fc

    def fill(out, pattern, base):
        return G(g.iota, [], out, pattern, base, 0, allow_small_or_imprecise_dtypes=True)

    gs = fill(T.sc[:, 1728:2048], [[0, 320]], 0)
    c0 = V(ms, [], T.sc[:, 0:864], 0.0)
    uz = V(ms, [], T.ut[:, 8:512], 0.0)
    b3 = V(ts, [gp], ic[:, 2:3], ic[:, 1:2], 7, None, A.bitwise_and)
    b5 = V(ts, [gp], ic[:, 4:5], ic[:, 0:1], 31, None, A.bitwise_and)
    b4 = V(ts, [gp], ic[:, 3:4], ic[:, 0:1], 3, None, A.logical_shift_right)
    sz = S([c0], T.sc[:, 864:1728], T.sc[:, 0:864], F.Copy)

    def scores(deps, w, ws, ps):
        return MM(deps, ps, w, ws, T.uq[:], T.uqs[:])

    hc = [slice(OWN + HALF * k, OWN + HALF * k + HALF) for k in (0, 1)]
    q0 = [V(qz, [e0[0]], T.hw[:, hc[0]], T.hws[:, hc[0]], T.e0t[:, 0:512])]
    quq = V(qz, [uu, uz], T.uq[:], T.uqs[:], T.ut[:])
    b6 = V(tc, [b3, b4, b5], fc[:, 0:3], ic[:, 2:5])
    q0.append(V(qz, [e0[1]], T.hw[:, hc[1]], T.hws[:, hc[1]], T.e0t[:, 512:1024]))
    for k in (0, 1):
        m = scores([q0[k], quq], T.hw[:, hc[k]], T.hws[:, hc[k]], T.ps[:, 512 * k:512 * k + 128])
    g0 = V(tc, [m], T.g0c[:], T.ps[:, 0:1024:512])

    def scales_out(k, a, b, es=inner):
        call([q0[k]], [("hk", es, T.hws[:, hc[k]], to[k][a:b], [T.hrs[:]] * (b - a))], "l0")

    scales_out(0, 0, 1, engs)
    call([g0], [("r0", engs, T.g0c[:], all_, [T.sld1[rel(d, i)] for i in others])])
    scales_out(1, 0, 2)
    scales_out(0, 1, 3)
    call([], [("hc", (inner, engs)[k], T.hw[:, hc[k]].bitcast(u8), to[k][0:1], [T.hr[:].bitcast(u8)]) for k in (0, 1)], "l0")
    scales_out(1, 2, 3)
    og = D("y", [g0], "dog0", T.sld1[N - 1], T.g0c[:])
    jz = fill(T.jt[:, 0:8], [[0, 8]], 0)
    xz = fill(T.xw[:], [[0, 128]], 0)
    t0 = [fill(T["tg%d" % t][:, 0:32], [[0, 32]], 0) for t in (1, 2)]
    rsb = fill(T.rsb[:], [[0, 16], [-8448, 16]], 8192)

    def col(deps, k, j, scale, bias, func=F.Identity):
        return S(deps, fc[:, k:k + 1], fc[:, j:j + 1], func, scale=scale, bias=bias)

    c4 = col([b6], 3, 0, 1.0, -6.0, F.Relu)
    c1 = col([b6], 5, 0, -GAP * U, 0.0)
    cm = col([b6], 4, 0, GAP, MAGIC)
    c5 = col([c4], 9, 3, 64.0, 0.0)
    nb = col([c4, c1], 6, 3, 7 * GAP * U, fc[:, 5:6])

    w = slice(0, 127)
    x = V(ts, [p1, p2], T.pa[:, w], T.pt[:, B0:B0 + 127], float(2048 - P * (d + 1)), 2.0, A.add, A.mult)
    r1 = V(ms, [], T.rs[:], BIG)
    jt = V(ts, [b6, giy], T.jt[:, 8:16], T.iy[:, 0:16:2], fc[:, 2:3], 2048.0, A.add, A.mult)
    dup = V(ts, [b6, giy], T.dup[:], T.iy[:], fc[:, 2:3], None, A.add)
    a1 = V(ts, [x], T.lo[:, w], T.pa[:, w], 254, None, A.bitwise_and)
    a2 = V(ts, [x], T.hb[:, w], T.pa[:, w], 8, 1, A.logical_shift_right, A.bitwise_and)
    a3 = V(ts, [x], T.wq2[:, w], T.pa[:, w], 1, OWN, A.logical_shift_right, A.bitwise_and)
    a4 = V(ts, [x], T.np[:, w], T.pa[:, w], 1, 2047, A.logical_shift_right, A.bitwise_and)
    a5 = V(tt, [a1, a2], T.tl[:, w], T.lo[:, w], T.hb[:, w], A.add)
    a6 = V(ts, [a3], T.wg[:, w], T.wq2[:, w], GAP / P, None, A.mult)
    a7 = V(tt, [a5, a3], T.s2[:, w], T.tl[:, w], T.wq2[:, w], A.add)
    a8 = V(tt, [a6, a4], T.s2[:, 128:255], T.wg[:, w], T.np[:, w], A.add)
    j2 = S([jt, jz], T.jt[:, 16:32], T.jt[:, 0:16], F.Identity, bias=-7 * GAP)
    rs = V(ms, [r1], T.rs[:, 0:32:4], -BIG)
    l1 = V(ts, [c5, gix], T.l1[:], T.ix[:], fc[:, 9:10], None, A.add)
    for y in (0, 2, 4, 6):
        x1 = V(tp, [a7, a8], T.t1[:, 16 * y:16 * y + 32], T.s2[:, y:256:8])
    zr = V(ms, [], T.zer[:], 0.0)
    for k in range(4):
        u, pi = k // 2, k % 2
        x2 = V(tc, [x1], T.t2[:, 32 * k:32 * k + 32], T.t1[:, 64 * u + pi:64 * u + 64:2])
    for k in range(4):
        xn = V(tp, [x1], T.nt[:, 32 * k:32 * k + 32], T.t1[:, k:128:4])
    for k in range(4):
        u, ka = k // 2, k % 2
        xd = V(tp, [x2], T.dl[:, 32 * k:32 * k + 32], T.t2[:, 64 * u + ka:64 * u + 64:2])
    for k in range(3):
        V(tt, [xn], T.vd[:, k:64:4], T.nt[:, 32 * k + 16:32 * k + 32], T.nt[:, 32 * k + 48:32 * k + 64], A.subtract)
    V(tt, [xn, j2], T.vd[:, 3:64:4], T.nt[:, 112:128], T.jt[:, 0:16], A.add)
    for k in range(4):
        u, ka = k // 2, k % 2
        ops = V(tc, [xd], T.op[:, 2 * ka + u:64:4], T.dl[:, 32 * k:32 * k + 16])
    vd = V(tt, [xn, xz], T.xw[:, 67:128:4], T.nt[:, 16:32], T.jt[:, 16:32], A.add)
    qa = []

    def tile_a(i):
        if len(qa) == i:
            qa.append(V(qz, [da], T.aq[:, 128 * i:128 * i + 128], T.aqs[:, 128 * i:128 * i + 128], T.at[:, 512 * i:512 * i + 512]))

    def places(dep, n, lo, tl, hm, po, out):
        a1 = V(ts, [dep], lo, n, 255, None, A.bitwise_and)
        yield None
        a3 = V(tt, [a1], tl, n, lo, A.add)
        a4 = V(ts, [a1], hm, lo, float(HALF), -255.0, A.is_ge, A.mult)
        yield None
        a5 = V(tt, [a3, a4], po, tl, hm, A.add)
        yield None
        yield V(tc, [a5], out, po)

    def spread(land, deps, sems):
        for k in range(8):
            D("ys"[k % 2], deps, sems[k % 2 if k else -1], T.sc[16 * k:16 * k + 1, :], land[:])
        return [(n, total[n]) for n in sems]

    def choose(t, deps):
        ga, tg, mx, fl, xd, xr = [T[n + str(t)] for n in ("ga", "tg", "mx", "fl", "xd", "xr")]
        o = 32 * t - 32
        x1 = V(tc, deps + [ops], ga[:, 0:192], T.sc[:].indirect(T.op[:, o:o + 12]))
        x2 = S(deps + [ops], ga[:, 192:512], T.sc[:].indirect(T.op[:, o + 12:o + 32]), F.Copy)
        tile_a(0)
        V(tp, [x1], tg[:, 32:224], ga[:, 0:192])
        x = V(tp, [x2], tg[:, 224:544], ga[:, 192:512])
        tile_a(1)
        x = V(scan, [x, rs, t0[1]], mx[:], tg[:, 16:528:16], T.rs[:], -BIG, A.max, A.min)
        tile_a(2)
        x = V(tt, [x], fl[:], tg[:, 32:544:16], mx[:], A.is_le)
        tile_a(3)
        x = V(scan, [x, vd], T.xw[:, o:o + 32], fl[:], T.vd[:, o:o + 32], 0.0, A.mult, A.add)
        y1 = V(tc, [x, l1], xd[:, 0:96], T.xw[:, o:128].indirect(T.l1[:, 0:6]))
        y2 = S([x, l1], xd[:, 96:256], T.xw[:, o:128].indirect(T.l1[:, 6:16]), F.Copy)
        z1 = V(tp, [y1], xr[:, 0:96], xd[:, 0:96])
        z2 = V(tp, [y2], xr[:, 96:256], xd[:, 96:256])
        for z, c in ((z1, slice(0, 96)), (z2, slice(96, 256))):
            mk = V(ts, [z, cm], T["mk%d" % t][:, c], xr[:, c], MAGIC, fc[:, 4:5], A.add, A.is_equal)
        return z2, mk, x1, x2

    def values(t, dep):
        return S([dep, nb, dup], T["bd%d" % t][:], T["xr%d" % t][:].indirect(T.dup[:]), F.Abs, bias=fc[:, 6:7], scale=U)

    def back(t, deps, op):
        yy, yt, mr = [T[n + str(t)] for n in ("yy", "yt", "mr")]
        c = [slice(HALF * k, HALF * k + HALF) for k in (0, 1)]
        x = [V(tt, deps, yy[:, c[k]], T["ct%d" % t][:].indirect(T.dup[:, 8 * k:8 * k + 8]), T["bd%d" % t][:, c[k]], op) for k in (0, 1)]
        x = [V(tp, [x[k]], yt[:, c[k]], yy[:, c[k]]) for k in (0, 1)]
        return [V(scan, [x[k], rsb], mr[:, c[k]], T.rsb[:, c[k]], yt[:, c[k]], BIG, A.max, A.min) for k in (0, 1)]

    def states(o, od, w, ws, x, xs, banks, h, tm, et, edep, q, qs, steps, nv):
        c = [slice(HALF * k, HALF * k + HALF) for k in (0, 1)]
        pc, pk = [], []
        for k in (0, 1):
            pc.append(V(tc, od[k], x[:, c[k]].bitcast(u32), w.bitcast(u32).indirect(o[:, 8 * k:8 * k + 8])))
            pk.append(S(od[k], xs[:, c[k]], ws.indirect(o[:, 8 * k:8 * k + 8]), F.Copy))
            next(steps)
        m, s, a, out = {}, {}, {}, []
        for k in (0, 1):
            for i in range(4):
                m[k, i] = MM([pc[k], pk[k]] + qa, banks[k][:, 512 * i:512 * i + HALF], T.aq[:, 128 * i:128 * i + 128], T.aqs[:, 128 * i:128 * i + 128],
                             x[:, c[k]], xs[:, c[k]])

        def scale(k, i):
            to_, r = tm[:, 512 * k + 128 * i:512 * k + 128 * i + 128], banks[k][:, 512 * i:512 * i + HALF]
            s[k, i] = V(ts, [m[k, i]], to_, r, 0.05, None, A.mult) if 4 * k + i < nv else S([m[k, i]], to_, r, F.Copy, scale=0.05)

        for n in range(6):
            scale(n // 4, n % 4)
            if n == 0:
                next(steps)
        for n in range(8):
            k, i = n // 4, n % 4
            e = slice(512 * k + i, 512 * k + 512, 4)
            a[n] = V(tt, [s[k, i], edep], h[:, e], tm[:, 128 * n:128 * n + 128], et[:, e], A.add)
            if n < 2:
                next(steps)
            if n == 1:
                scale(1, 2)
                scale(1, 3)
            if n in (4, 7):
                k = n // 7
                out.append(V(qz, [a[4 * k + 3]], q[:, c[k]], qs[:, c[k]], h[:, 512 * k:512 * k + 512]))
        return out

    got = spread(T.sld1, [og, ("r0", 7 * neng), sz, gs], ("ds0", "ds1", "dsx"))
    there = slice(P * rel(d, mate), P * rel(d, mate) + P)
    call(got[2:], [("hh", engs, T.hw[:, OWN:OWN + P].bitcast(u8), [cores[mate]], [T.hw[:, there].bitcast(u8)])], "l0")
    call([], [("hh", engs, T.hws[:, OWN:OWN + P], [cores[mate]], [T.hws[:, there]])], "l0")
    giz = G(g.iota, [], T.iz[:], [[16, 16]], 0, 0)
    ch, mk, g0v, g0s = choose(1, got)
    e1 = D("y", [g0v], "de1", T.e1t[:], T.e1[:, :])
    bv = values(1, ch)
    x = V(scan, [mk, zr], T.ct1[:], T.mk1[:], T.zer[:], -float(CAP), A.add, A.add)
    z = back(1, [x, bv], A.max)
    o1 = [V(ts, [z[k]], T.ofx1[:, 8 * k:8 * k + 8], T.mr1[:, 7 + HALF * k:HALF + HALF * k:16], 4096.0, None, A.mult) for k in (0, 1)]
    arr = [("hh", (6 * 4 + 2) * neng), g0]
    tj = T.tj
    sr1 = []

    def chosen_scores():
        sr1.append(V(ts, z, tj[:, 0:16], T.mr1[:, 7:256:16], 4096.0, None, A.mult))
        yield None
        for k, os1 in enumerate(places(sr1[0], tj[:, 0:16], tj[:, 16:32], tj[:, 48:64], tj[:, 64:80], tj[:, 80:96], T.ofs1[:])):
            if k < 3:
                yield None
        sr1.append(S([os1], T.scr1[:], T.sc[:].indirect(T.ofs1[:]), F.Copy))
        for k in (0, 1):
            scc = D("y", sr1[1:2], "dsc", T.scc[:, k:k + 1], T.scr1[0:1, HALF * k:HALF * k + HALF])
        sr1.append(scc)
        yield None

    q1 = states(T.ofx1, [[o] + arr for o in o1], T.hw[:], T.hws[:], T.x1, T.x1s, (T.pr, T.ps), T.h1, T.tm1, T.e1t, e1, T.hq, T.hqs, chosen_scores(), 1)
    for k in (0, 1):
        mg = scores([q1[k]], T.hq[:, HALF * k:HALF * k + HALF], T.hqs[:, HALF * k:HALF * k + HALF], T.pr[:, 512 * k:512 * k + 128])
    g1 = V(tt, [mg, sr1[2]], T.g1c[:], T.pr[:, 0:1024:512], T.scc[:], A.add)

    call([g1], [("rg", engs, T.g1c[:], all_, [T.sld2[rel(d, i)] for i in others])])
    og = D("y", [g1], "dog1", T.sld2[N - 1], T.g1c[:])
    c2 = col([], 7, 0, -2.0, 0.0)
    c6 = col([], 10, 3, CAP + 0.5, -float(CAP))
    for k in (0, 1):
        c7 = S([], T.cq[:, 264 * k:264 * k + 1], fc[:, 1:2], F.Identity, bias=0.5 + 16 * k)
    q1b = V(qz, q1, T.w2[:, P:2 * P], T.w2s[:, P:2 * P], T.h1[:])
    x = V(ts, [gp], ic[:, 5:6], ic[:, 0:1], 15, None, A.bitwise_and)
    x = V(tc, [x], fc[:, 12:13], ic[:, 5:6])
    jo = V(ts, [x, giz], T.jo[:], T.iz[:], fc[:, 12:13], -0.5, A.add, A.mult)

    def absolute(x, n, a, b, out):
        x = V(ts, [x], a, n, float(P * (d + 1)), None, A.add)
        x = V(ts, [x], b, a, 2047, None, A.bitwise_and)
        return V(tc, [x], out, b)

    oa1 = absolute(sr1[0], tj[:, 0:16], tj[:, 144:160], tj[:, 160:176], T.cf[:, 0:16])
    got = spread(T.sld2, [og, ("rg", 7 * neng), g0v, g0s, sr1[1]], ("ds3", "ds2", "ds3"))
    e2 = D("y", got, "de2", T.e2t[:], T.e2[:, :])
    dw = D("y", [], "dw", T.wt[:], T.w[:, :])

    ch, mk = choose(2, got)[0:2]
    y = S([ch, c2], T.b2[:], T.xr2[:], F.Abs, bias=fc[:, 7:8], scale=2.0 / GAP)
    bv = values(2, ch)
    x = [V(scan, [mk, zr, c7], T.cq[:, 264 * k + 1:264 * k + 257], T.zer[:], T.mk2[:], T.cq[:, 264 * k:264 * k + 1], A.add, A.subtract) for k in (0, 1)]
    sel = [V(scan, [x[k], y], T.zz[:, P * k:P * k + P], T.cq[:, 264 * k:264 * k + 256], T.b2[:], 0.0, A.max, A.min) for k in (0, 1)]
    x = V(ts, sel, T.rv[:, 0:2], T.zz[:, 255:512:256], GAP / 2.0, None, A.mult)
    cnt = V(scan, [mk, c6], T.ct2[:], T.mk2[:], T.zer[:], fc[:, 10:11], A.add, A.add)
    x = V(ts, [x], T.rv[:, 2:4], T.rv[:, 0:2], 255, None, A.bitwise_and)
    rq = V(tc, [x], T.rq[:], T.rv[:, 2:4])
    call([rq], [("rr", engs, T.rq[:], all_, [T.rqs[:, 2 * j:2 * j + 2] for j in [seats(i, cores, topo).index(d) for i in others]])])
    for k in range(8):
        D("ys"[k % 2], [("rr", 7 * neng)], ("dofq", "dofs")[k % 2], T.ofq[16 * k:16 * k + 16, 0:14], T.rqs[d:128:8, 0:14])
    oq = [("dofq", 64), ("dofs", 64)]
    z = back(2, [cnt, bv], A.add)
    ti = T.ti
    x = V(tt, z + [jo], T.b2[:, 0:16], T.mr2[:, 7:256:16], T.jo[:], A.add)
    qw = V(qz, [dw], T.wq[:], T.wqs[:], T.wt[:])
    zi = V(ts, [x], ti[:, 0:16], T.b2[:, 0:16], float(CAP), 4096.0, A.add, A.mult)
    cf = V(ts, [zi], ti[:, 16:32], ti[:, 0:16], 2047, None, A.bitwise_and)
    k1 = V(ts, [zi], ti[:, 32:48], ti[:, 0:16], 12, None, A.logical_shift_right)
    k2 = V(ts, [zi], ti[:, 48:64], ti[:, 0:16], 3, CAP * (N - 1), A.logical_shift_right, A.bitwise_and)
    pc = V(tc, oq + q1, T.sp[:].bitcast(u32), T.hq[:].bitcast(u32).indirect(T.ofq[:, 0:14]))
    pk = S(oq + q1, T.sps[:], T.hqs[:].indirect(T.ofq[:, 0:14]), F.Copy)
    call([pk], [("hz", inner[4 * k:4 * k + 4], T.sps[:, 96 * k:96 * k + 128], [to[0][k]], [T.hs[:, 96 * k:96 * k + 128]]) for k in (0, 1)])
    call([pc], [("rc", engs[k:k + 1], T.sp[:, CAP * k:CAP * k + CAP].bitcast(u8), [cores[i]],
                 [T.w2[:, CAP * rel(d, i):CAP * rel(d, i) + CAP].bitcast(u8)]) for k, i in enumerate(seats(d, cores, topo))])
    k3 = V(ts, [cf], ti[:, 64:80], ti[:, 16:32], float(1 - OWN), 0.0, A.add, A.max)
    k4 = V(tt, [k1, k2], ti[:, 80:96], ti[:, 32:48], ti[:, 48:64], A.add)
    k5 = V(tt, [k3, k4], ti[:, 96:112], ti[:, 64:80], ti[:, 80:96], A.add)
    ox2 = V(ts, [k5], T.ofx2[:], ti[:, 96:112], -1.0, None, A.add)
    os2 = list(places(cf, ti[:, 16:32], tj[:, 96:112], tj[:, 128:144], tj[:, 208:224], tj[:, 224:240], T.ofs2[:]))[-1]
    oa2 = absolute(cf, ti[:, 16:32], tj[:, 176:192], tj[:, 192:208], T.cf[:, 16:32])
    sr2 = S([os2], T.scr2[:], T.sc[:].indirect(T.ofs2[:]), F.Copy)
    x = V(tp, [oa1, oa2], T.cht[:], T.cf[:])
    D("y", [x], "dout", T.ch[:, :], T.cht[0:32, 0:16])

    q2 = states(T.ofx2, [[("rc", 7 * 3), ox2, q1b, g1]] * 2, T.w2[:], T.w2s[:], T.x2, T.x2s, (T.ps, T.pr), T.h2, T.tm2, T.e2t, e2, T.zq, T.zqs,
                iter(range(9)), 2)
    for k in (0, 1):
        c = slice(HALF * k, HALF * k + HALF)
        m1 = MM([q2[k], qw], T.ps[:, 512 * k:512 * k + HALF], T.wq[:], T.wqs[:], T.zq[:, c], T.zqs[:, c])
        m2 = MM([q2[k]], T.ps[:, 1024 + 512 * k:1024 + 512 * k + HALF], T.uq[:], T.uqs[:], T.zq[:, c], T.zqs[:, c])
        D("y", [q2[k]], "dout", T.oc[:, 4 * HALF * k:4 * HALF * (k + 1)], T.zq[:, c].bitcast(u8))
        yy = V(tc, [m1], T.ys[:, c], T.ps[:, 512:512 + HALF]) if k else S([m1], T.ys[:, c], T.ps[:, 0:HALF], F.Copy)
        gg = V(tt, [m2, sr2], T.go[0:1, c], T.ps[0:1, 1024 + 512 * k:1024 + 512 * k + HALF], T.scr2[0:1, c], A.add)
        if k:
            for i in range(4):
                D("y", [q2[k]], "dout", T.osc[4 * i:4 * i + 4, :], T.zqs[32 * i:32 * i + 4, :])
        D("s", [yy], "dch", T.y[:, c], T.ys[:, c])
    D("y", [gg], "dout", T.g[0:1, :], T.go[0:1, :])

    wait("g", [(n, total[n]) for n in total])
